import numpy as np
import ml_dtypes


def mxq(x, axis, fmt="e4m3"):
    dtype, down = {"e4m3": (ml_dtypes.float8_e4m3fn, 7), "e5m2": (ml_dtypes.float8_e5m2, 14)}[fmt]
    v = np.moveaxis(np.asarray(x, np.float32).astype(ml_dtypes.bfloat16).astype(np.float64), axis, -1)
    blocks = v.reshape(v.shape[:-1] + (-1, 32))
    amax = np.abs(blocks).max(-1, keepdims=True)
    byte = np.maximum(np.where(amax > 0, np.frexp(amax)[1] - 1 + 127, 0) - down, 1)
    scale = np.exp2(byte - 127.0)
    codes = (blocks / scale).astype(np.float32).astype(dtype).astype(np.float64)
    return np.moveaxis((codes * scale).reshape(v.shape), -1, axis)


WIDE = False


def mx_kscale(k):
    if not WIDE:
        return np.ones(k)
    levels = np.array([24, -24, 12, -12, 0])
    if k % 512:
        return np.exp2(np.random.permutation(np.resize(levels, k // 32))).repeat(32)
    a = np.empty((k // 512, 16))
    for p in range(k // 512):
        a[p, :8] = np.random.permutation(np.resize(levels, 8))
        for g in range(8):
            far = levels[np.abs(levels - a[p, g]) >= 10]
            a[p, g + 8] = far[np.random.randint(len(far))]
    return np.exp2(a.ravel()).repeat(32)


def f64(x):
    return np.asarray(x).astype(np.float64)


def striped(idx):
    return np.tile(idx.reshape(-1, 16).T, (8, 1)).astype(np.uint16)


def unstriped(offs):
    return offs[:16].T.reshape(-1).astype(np.int64)


E2M1 = np.array([0.0, 0.5, 1.0, 1.5, 2.0, 3.0, 4.0, 6.0, -0.0, -0.5, -1.0, -1.5, -2.0, -3.0, -4.0, -6.0])


def pack_weight(w, fmt):
    k, n = w.shape
    w = f64(np.asarray(w, np.float32).astype(ml_dtypes.bfloat16)).reshape(k // 32, 32, n)
    amax = np.abs(w).max(1)
    if fmt == "e4m3":
        byte = np.frexp(amax)[1] - 1 + 127 - 7
    else:
        mant, ex = np.frexp(amax / 6.0)
        byte = np.where(mant > 0.5, ex, ex - 1) + 127
    byte = np.clip(np.where(amax > 0, byte, 1), 1, 254)
    scaled = (w * np.exp2(127.0 - byte)[:, None, :]).reshape(k, n).astype(np.float32)
    by_word = np.ascontiguousarray(scaled.reshape(k // 512, 128, 4, n).transpose(0, 1, 3, 2))
    if fmt == "e4m3":
        words = by_word.astype(ml_dtypes.float8_e4m3fn).view(np.uint8)
    else:
        c = by_word.astype(ml_dtypes.float4_e2m1fn).view(np.uint8) & 0xF
        words = (c[..., 0::2] | (c[..., 1::2] << 4)).reshape(k // 512, 128, 2 * n)
    return np.ascontiguousarray(words), np.ascontiguousarray(byte.astype(np.uint8).reshape(k // 512, 16, n))


def unpack_weight(words, scales, fmt):
    g, _, n = scales.shape
    words = np.ascontiguousarray(words).reshape(g, 128, n, -1)
    if fmt == "e4m3":
        vals = words.view(ml_dtypes.float8_e4m3fn).astype(np.float64)
    else:
        nib = np.empty((g, 128, n, 4), np.uint8)
        nib[..., 0::2] = words & 0xF
        nib[..., 1::2] = words >> 4
        vals = E2M1[nib]
    vals = vals * np.repeat(np.exp2(scales.astype(np.float64) - 127.0), 8, axis=1)[..., None]
    return vals.transpose(0, 1, 3, 2).reshape(g * 512, n)


def pack_table4(v):
    words, scales = pack_weight(v, "e2m1")
    g, t = words.shape[0] // 2, v.shape[1]
    return np.ascontiguousarray(words.reshape(g, 2, 128, t, 2).transpose(0, 2, 3, 1, 4).reshape(g, 128, t, 4)), scales


def unpack_table4(words, scales):
    g, _, t, _ = words.shape
    return unpack_weight(words.reshape(g, 128, t, 2, 2).transpose(0, 3, 1, 2, 4).reshape(2 * g, 128, 2 * t), scales, "e2m1")


def silu(f):
    return f / (1.0 + np.exp(-np.maximum(f, -700.0)))


def sigm(f):
    return 1.0 / (1.0 + np.exp(-np.maximum(f, -700.0)))


K, L, N, T, J = 1024, 512, 512, 2048, 1024


def setup_inputs():
    n = np.random.standard_normal
    s = mx_kscale(K)[:, None]
    s2 = mx_kscale(L)[:, None]
    p_tab = pack_table4(n((K, T)) * s)
    p_tab2 = pack_weight(n((L, T)) * s2, "e4m3")
    p_zv = pack_weight(n((K, N)) / np.sqrt(K) / s, "e2m1")
    p_zt = pack_weight(n((L, N)) / np.sqrt(L) / s2, "e2m1")
    p_wv = pack_weight(n((K, N)) / np.sqrt(K) / s, "e2m1")
    return {
        "tab_words": p_tab[0],
        "tab_scales": p_tab[1],
        "tab2_words": p_tab2[0],
        "tab2_scales": p_tab2[1],
        "zv_words": p_zv[0],
        "zv_scales": p_zv[1],
        "zt_words": p_zt[0],
        "zt_scales": p_zt[1],
        "b": (0.3 * n(N)).astype(np.float32),
        "wv_words": p_wv[0],
        "wv_scales": p_wv[1],
        "wt": (n((L, N)) / np.sqrt(L) / s2).astype(np.float32),
        "rT": (n((N, T))).astype(np.float32),
        "offs": striped(np.random.permutation(T)[:J]),
        "offs2": striped(np.random.permutation(T)[:J]),
    }


def reference(tab_words, tab_scales, tab2_words, tab2_scales, zv_words, zv_scales, zt_words, zt_scales, b, wv_words, wv_scales, wt, rT, offs, offs2):
    idx = unstriped(offs)
    idx2 = unstriped(offs2)
    tab_ = unpack_table4(tab_words, tab_scales)[:, idx]
    tab2_ = unpack_weight(tab2_words, tab2_scales, "e4m3")[:, idx2]
    zv_ = unpack_weight(zv_words, zv_scales, "e2m1")
    zt_ = unpack_weight(zt_words, zt_scales, "e2m1")
    z = zv_.T @ tab_ + zt_.T @ tab2_
    gate = sigm(z + f64(b)[:, None])
    wv_ = unpack_weight(wv_words, wv_scales, "e2m1")
    wt_ = mxq(f64(wt), 0, "e4m3")
    hv = wv_.T @ tab_
    ht = wt_.T @ tab2_
    av = silu(hv)
    at = silu(ht)
    return at + gate * (av - at) + f64(rT)[:, idx]

@@ -1,0 +1,258 @@
+from contextlib import ExitStack
+
+import concourse.mybir as mybir
+from concourse.masks import make_identity
+
+K, L, N, T, J = 1024, 512, 512, 2048, 1024
+FLOPS = 2 * N * J * (2 * K + 2 * L)
+
+F32 = mybir.dt.float32
+BF16 = mybir.dt.bfloat16
+I32 = mybir.dt.int32
+U32 = mybir.dt.uint32
+U16 = mybir.dt.uint16
+U8 = mybir.dt.uint8
+FP8X4 = mybir.dt.float8_e4m3fn_x4
+FP4X4 = mybir.dt.float4_e2m1fn_x4
+ACT = mybir.ActivationFunctionType
+ALU = mybir.AluOpType
+
+P = 128
+H = 512
+NT = N // P
+JT = H // P
+
+
+def tile_list_gmu_silu_resL_kernel(
+    tc, tab_words, tab_scales, tab2_words, tab2_scales, zv_words, zv_scales, zt_words, zt_scales,
+    b, wv_words, wv_scales, wt, rT, offs, offs2, out,
+):
+    nc = tc.nc
+    with ExitStack() as ctx:
+        lists = ctx.enter_context(tc.tile_pool(name="lists", bufs=1))
+        keep = ctx.enter_context(tc.tile_pool(name="keep", bufs=1))
+        psum = ctx.enter_context(tc.psum_pool(name="psum", bufs=1))
+
+        def sb(name, shape, dtype):
+            return keep.tile(shape, dtype, name=name, align_bytes=64)
+
+        idx = lists.tile([P, J // 16], U16, name="idx")
+        idx2 = lists.tile([P, J // 16], U16, name="idx2")
+
+        tabs = sb("tabs", [P, T // 4], I32)
+        tab2s = sb("tab2s", [P, T // 4], I32)
+        wsc = sb("wsc", [P, 5, N // 4], I32)
+        tabw = sb("tabw", [P, T], I32)
+        tab2w = sb("tab2w", [P, T], I32)
+        wvw = sb("wvw", [P, 2, N // 2], I32)
+        zvw = sb("zvw", [P, 2, N // 2], I32)
+        ztw = sb("ztw", [P, N // 2], I32)
+        wt_raw = [sb(f"wt_raw{c}", [P, 4, N // 2], F32) for c in range(2)]
+        wt_bf = [sb(f"wt_bf{c}", [P, N // 2, 4], BF16) for c in range(2)]
+        wtq = sb("wtq", [P, N], U32)
+        wts = sb("wts", [P, N], U8)
+        r_win = [sb(f"r_win{t}", [P, T], F32) for t in range(NT)]
+        b_col = sb("b_col", [P, NT], F32)
+        b_half = sb("b_half", [P, NT], F32)
+        ident = sb("ident", [P, P], F32)
+        warm = sb("warm", [P, 8], F32)
+        warm_o = sb("warm_o", [P, 8], F32)
+
+        gs = [sb(f"gs{h}", [P, H], U8) for h in range(2)]
+        gs1 = [sb(f"gs1_{h}", [P, H // 4], I32) for h in range(2)]
+        gs2 = [sb(f"gs2_{h}", [P, H], U8) for h in range(2)]
+        gw = [sb(f"gw{h}", [P, H], U32) for h in range(2)]
+        gsp = [sb(f"gsp{h}", [P, 2, H], U16) for h in range(2)]
+        gw2 = [sb(f"gw2_{h}", [P, H], U32) for h in range(2)]
+        av = [sb(f"av{i}", [P, N], F32) for i in range(2 * JT)]
+        at = [sb(f"at{i}", [P, N], F32) for i in range(2 * JT)]
+        dd = [sb(f"dd{i}", [P, N], F32) for i in range(2 * JT)]
+        ee = [sb(f"ee{i}", [P, N], F32) for i in range(2 * JT)]
+        th = [[sb(f"th{h}_{t}", [P, H], F32) for t in range(NT)] for h in range(2)]
+        rg = [[sb(f"rg{h}_{t}", [P, H], F32) for t in range(NT)] for h in range(2)]
+        res = [[sb(f"res{h}_{t}", [P, H], F32) for t in range(NT)] for h in range(2)]
+
+        def cols(h):
+            return slice(h * (H // 16), (h + 1) * (H // 16))
+
+        nc.vector.memset(tabs[:], 0)
+        nc.vector.memset(wsc[:], 0)
+        for h in range(2):
+            nc.vector.memset(gs1[h][:], 0)
+        nc.vector.memset(warm[:], 0.0)
+        nc.scalar.activation(warm_o[:], warm[:], ACT.Silu)
+        with nc.allow_non_contiguous_dma(reason="bias onto partitions"):
+            nc.gpsimd.dma_start(out=b_col[:], in_=b.rearrange("(t p) -> p t", p=P))
+        make_identity(nc, ident[:])
+
+        def load_scales(eng, dst, src, q):
+            eng.dma_start(out=dst, in_=src[:, 4 * q : 4 * q + 4, :].rearrange("a r n -> r a n").bitcast(I32))
+
+        wt_v = wt.rearrange("(p j) n -> p j n", j=4)
+        tab_rows = tab_scales.rearrange("a (q r) t -> r q a t", r=4)
+        nc.sync.dma_start(idx2[:], offs2)
+        for q in range(4):
+            rows = tab2_scales[0, 4 * q : 4 * q + 4, :].bitcast(I32)
+            nc.sync.dma_start(out=tab2s[32 * q : 32 * q + 32, :], in_=rows.unsqueeze(0).to_broadcast([8, 4, T // 4]))
+        nc.sync.dma_start(out=tab2w[:], in_=tab2_words[0].rearrange("p t b -> p (t b)").bitcast(I32))
+        nc.sync.dma_start(out=wt_raw[0][:], in_=wt_v[:, :, 0 : N // 2])
+        nc.sync.dma_start(out=wt_raw[1][:], in_=wt_v[:, :, N // 2 : N])
+        nc.sync.dma_start(idx[:], offs)
+        for r in range(4):
+            nc.sync.dma_start(out=tabs[r:P:16, :], in_=tab_rows[r].bitcast(I32))
+        nc.sync.dma_start(out=tabw[:], in_=tab_words[0].rearrange("p t b -> p (t b)").bitcast(I32))
+        nc.sync.dma_start(out=wvw[:], in_=wv_words.rearrange("a p n -> p a n").bitcast(I32))
+        for q in range(4):
+            load_scales(nc.sync, wsc[32 * q : 32 * q + 4, 0:2, :], wv_scales, q)
+        nc.sync.dma_start(out=zvw[:], in_=zv_words.rearrange("a p n -> p a n").bitcast(I32))
+        nc.sync.dma_start(out=ztw[:], in_=zt_words[0].bitcast(I32))
+        nc.sync.dma_start(out=r_win[0][:], in_=rT[0:P, :])
+        for q in range(4):
+            load_scales(nc.sync, wsc[32 * q : 32 * q + 4, 2:4, :], zv_scales, q)
+        for q in range(4):
+            nc.sync.dma_start(out=wsc[32 * q : 32 * q + 4, 4, :], in_=zt_scales[0, 4 * q : 4 * q + 4, :].bitcast(I32))
+        for t in range(1, NT):
+            nc.sync.dma_start(out=r_win[t][:], in_=rT[t * P : (t + 1) * P, :])
+
+        nc.scalar.activation(b_half[:], b_col[:], ACT.Copy, scale=0.5)
+
+        wsc8 = wsc[:].rearrange("p a n -> p (a n)").bitcast(U8)
+
+        def wplane(a, lo, hi):
+            return wsc8[:, a * N + lo : a * N + hi]
+
+        def gather_tab_scales(h):
+            nc.vector.tensor_copy(gs[h][:], tabs[:].bitcast(U8).indirect(idx[:, cols(h)]))
+            nc.gpsimd.dma_start(out=gs1[h][0:112, :], in_=gs[h][16:128, :].bitcast(I32))
+
+        def gather_tab_words(h):
+            nc.vector.tensor_copy(gw[h][:], tabw[:].bitcast(U32).indirect(idx[:, cols(h)]))
+
+        def split(h):
+            nc.vector.tensor_copy(gsp[h][:], gw[h][:].bitcast(U16).rearrange("p (t d) -> p d t", d=2))
+
+        def gather_tab2_words(h):
+            nc.vector.tensor_copy(gw2[h][:], tab2w[:].bitcast(U32).indirect(idx2[:, cols(h)]))
+
+        def gather_tab2_scales(h):
+            nc.vector.tensor_copy(gs2[h][:], tab2s[:].bitcast(U8).indirect(idx2[:, cols(h)]))
+
+        def tab_plane(h, a, lo, hi):
+            if a == 0:
+                return gs[h][:, lo:hi]
+            return gs1[h][:].bitcast(U8)[:, lo:hi]
+
+        def tab_codes(h, a, lo, hi):
+            return gsp[h][:, a, lo:hi].bitcast(FP4X4)
+
+        def bank(tag, bufs):
+            return psum.tile([P, 512], F32, name=tag, tag=tag, bufs=bufs)
+
+        def hv_unit(h, s):
+            acc = bank("mx", 4)
+            for a in range(2):
+                nc.tensor.matmul_mx(
+                    out=acc[:], lhsT=tab_codes(h, a, s * P, (s + 1) * P), lhsT_scale=tab_plane(h, a, s * P, (s + 1) * P),
+                    rhs=wvw[:, a, :].bitcast(FP4X4), rhs_scale=wplane(a, 0, N), start=(a == 0), stop=(a == 1),
+                )
+            i = h * JT + s
+            nc.scalar.activation(av[i][:], acc[:], ACT.Silu)
+            nc.gpsimd.tensor_tensor(dd[i][:], av[i][:], at[i][:], ALU.subtract)
+
+        def ht_unit(h, s):
+            acc = bank("mx", 4)
+            nc.tensor.matmul_mx(
+                out=acc[:], lhsT=gw2[h][:, s * P : (s + 1) * P].bitcast(FP8X4), lhsT_scale=gs2[h][:, s * P : (s + 1) * P],
+                rhs=wtq[:].bitcast(FP8X4), rhs_scale=wts[:], start=True, stop=True,
+            )
+            i = h * JT + s
+            nc.scalar.activation(at[i][:], acc[:], ACT.Silu)
+
+        def z_unit(h, t):
+            acc = bank("mx", 4)
+            for a in range(2):
+                nc.tensor.matmul_mx(
+                    out=acc[:], lhsT=zvw[:, a, t * 64 : (t + 1) * 64].bitcast(FP4X4), lhsT_scale=wplane(2 + a, t * P, (t + 1) * P),
+                    rhs=tab_codes(h, a, 0, H), rhs_scale=tab_plane(h, a, 0, H), start=(a == 0), stop=False,
+                )
+            nc.tensor.matmul_mx(
+                out=acc[:], lhsT=ztw[:, t * 64 : (t + 1) * 64].bitcast(FP4X4), lhsT_scale=wplane(4, t * P, (t + 1) * P),
+                rhs=gw2[h][:].bitcast(FP8X4), rhs_scale=gs2[h][:], start=False, stop=True,
+            )
+            nc.scalar.activation(th[h][t][:], acc[:], ACT.Tanh, bias=b_half[:, t : t + 1], scale=0.5)
+
+        def e_unit(h, s):
+            acc = bank("tt", 2)
+            for t in range(NT):
+                nc.tensor.transpose(acc[:, t * P : (t + 1) * P], th[h][t][:, s * P : (s + 1) * P], ident[:])
+            i = h * JT + s
+            nc.vector.scalar_tensor_tensor(ee[i][:], acc[:], 1.0, dd[i][:], ALU.add, ALU.mult)
+
+        def gather_r(h, t):
+            nc.vector.tensor_copy(rg[h][t][:], r_win[t][:].indirect(idx[:, cols(h)]))
+
+        def out_unit(h, t):
+            acc = bank("fin", 2)
+            for s in range(JT):
+                i = h * JT + s
+                terms = (at[i], at[i], ee[i])
+                for u in range(3):
+                    nc.tensor.matmul(
+                        acc[:, s * P : (s + 1) * P], terms[u][:, t * P : (t + 1) * P], ident[:],
+                        start=(u == 0), stop=(u == 2), is_transpose=True,
+                    )
+            nc.vector.scalar_tensor_tensor(res[h][t][:], acc[:], 0.5, rg[h][t][:], ALU.mult, ALU.add)
+            nc.sync.dma_start(out=out[t * P : (t + 1) * P, h * H : (h + 1) * H], in_=res[h][t][:])
+
+        def cast_wt(c):
+            nc.scalar.copy(wt_bf[c][:], wt_raw[c][:].rearrange("p j n -> p n j"))
+
+        def quantise_wt(c):
+            lo, hi = c * (N // 2), (c + 1) * (N // 2)
+            nc.vector.quantize_mx(out=wtq[:, lo:hi].bitcast(FP8X4), scales=wts[:, lo:hi], in_=wt_bf[c][:].rearrange("p n j -> p (n j)"))
+
+        cast_wt(0)
+        cast_wt(1)
+        gather_tab2_scales(0)
+        gather_tab2_scales(1)
+        gather_tab2_words(0)
+        gather_tab2_words(1)
+        quantise_wt(0)
+        quantise_wt(1)
+        for h in range(2):
+            for s in range(JT):
+                ht_unit(h, s)
+        gather_tab_scales(0)
+        gather_tab_scales(1)
+        gather_tab_words(0)
+        split(0)
+        for s in range(JT):
+            hv_unit(0, s)
+        gather_tab_words(1)
+        split(1)
+        for t in range(NT):
+            z_unit(0, t)
+        for s in range(JT):
+            hv_unit(1, s)
+        gather_r(0, 0)
+        gather_r(1, 0)
+        for t in range(NT):
+            z_unit(1, t)
+        gather_r(0, 1)
+        gather_r(1, 1)
+        for s in range(JT):
+            e_unit(0, s)
+        gather_r(0, 2)
+        gather_r(1, 2)
+        out_unit(0, 0)
+        out_unit(0, 1)
+        for s in range(JT):
+            e_unit(1, s)
+        out_unit(0, 2)
+        gather_r(0, 3)
+        out_unit(0, 3)
+        out_unit(1, 0)
+        gather_r(1, 3)
+        out_unit(1, 1)
+        out_unit(1, 2)
+        out_unit(1, 3)

@@ -58,9 +58,9 @@ def tile_list_gmu_silu_resL_kernel(
         warm = sb("warm", [P, 8], F32)
         warm_o = sb("warm_o", [P, 8], F32)
 
-        gs = [sb(f"gs{h}", [P, H], U8) for h in range(2)]
-        gs1 = [sb(f"gs1_{h}", [P, H // 4], I32) for h in range(2)]
-        gs2 = [sb(f"gs2_{h}", [P, H], U8) for h in range(2)]
+        gs = sb("gs", [P, J], U8)
+        gs1 = sb("gs1", [P, J // 4], I32)
+        gs2 = sb("gs2", [P, J], U8)
         gw = [sb(f"gw{h}", [P, H], U32) for h in range(2)]
         gsp = [sb(f"gsp{h}", [P, 2, H], U16) for h in range(2)]
         gw2 = [sb(f"gw2_{h}", [P, H], U32) for h in range(2)]
@@ -69,16 +69,16 @@ def tile_list_gmu_silu_resL_kernel(
         dd = [sb(f"dd{i}", [P, N], F32) for i in range(2 * JT)]
         ee = [sb(f"ee{i}", [P, N], F32) for i in range(2 * JT)]
         th = [[sb(f"th{h}_{t}", [P, H], F32) for t in range(NT)] for h in range(2)]
-        rg = [[sb(f"rg{h}_{t}", [P, H], F32) for t in range(NT)] for h in range(2)]
-        res = [[sb(f"res{h}_{t}", [P, H], F32) for t in range(NT)] for h in range(2)]
+        rg = [sb(f"rg{h}", [P, NT, H], F32) for h in range(2)]
+        res = [sb(f"res{t}", [P, H], F32) for t in range(NT)]
+        res_j = [sb(f"res_j{s}", [P, NT, P], F32) for s in range(JT)]
 
         def cols(h):
             return slice(h * (H // 16), (h + 1) * (H // 16))
 
         nc.vector.memset(tabs[:], 0)
         nc.vector.memset(wsc[:], 0)
-        for h in range(2):
-            nc.vector.memset(gs1[h][:], 0)
+        nc.vector.memset(gs1[:], 0)
         nc.vector.memset(warm[:], 0.0)
         nc.scalar.activation(warm_o[:], warm[:], ACT.Silu)
         with nc.allow_non_contiguous_dma(reason="bias onto partitions"):
@@ -94,21 +94,21 @@ def tile_list_gmu_silu_resL_kernel(
         for q in range(4):
             rows = tab2_scales[0, 4 * q : 4 * q + 4, :].bitcast(I32)
             nc.sync.dma_start(out=tab2s[32 * q : 32 * q + 32, :], in_=rows.unsqueeze(0).to_broadcast([8, 4, T // 4]))
-        nc.sync.dma_start(out=tab2w[:], in_=tab2_words[0].rearrange("p t b -> p (t b)").bitcast(I32))
-        nc.sync.dma_start(out=wt_raw[0][:], in_=wt_v[:, :, 0 : N // 2])
-        nc.sync.dma_start(out=wt_raw[1][:], in_=wt_v[:, :, N // 2 : N])
         nc.sync.dma_start(idx[:], offs)
+        nc.sync.dma_start(out=wt_raw[0][:], in_=wt_v[:, :, 0 : N // 2])
         for r in range(4):
             nc.sync.dma_start(out=tabs[r:P:16, :], in_=tab_rows[r].bitcast(I32))
+        nc.sync.dma_start(out=tab2w[:], in_=tab2_words[0].rearrange("p t b -> p (t b)").bitcast(I32))
+        nc.sync.dma_start(out=wt_raw[1][:], in_=wt_v[:, :, N // 2 : N])
         nc.sync.dma_start(out=tabw[:], in_=tab_words[0].rearrange("p t b -> p (t b)").bitcast(I32))
-        nc.sync.dma_start(out=wvw[:], in_=wv_words.rearrange("a p n -> p a n").bitcast(I32))
         for q in range(4):
             load_scales(nc.sync, wsc[32 * q : 32 * q + 4, 0:2, :], wv_scales, q)
+        nc.sync.dma_start(out=wvw[:], in_=wv_words.rearrange("a p n -> p a n").bitcast(I32))
         nc.sync.dma_start(out=zvw[:], in_=zv_words.rearrange("a p n -> p a n").bitcast(I32))
-        nc.sync.dma_start(out=ztw[:], in_=zt_words[0].bitcast(I32))
-        nc.sync.dma_start(out=r_win[0][:], in_=rT[0:P, :])
         for q in range(4):
             load_scales(nc.sync, wsc[32 * q : 32 * q + 4, 2:4, :], zv_scales, q)
+        nc.sync.dma_start(out=r_win[0][:], in_=rT[0:P, :])
+        nc.sync.dma_start(out=ztw[:], in_=zt_words[0].bitcast(I32))
         for q in range(4):
             nc.sync.dma_start(out=wsc[32 * q : 32 * q + 4, 4, :], in_=zt_scales[0, 4 * q : 4 * q + 4, :].bitcast(I32))
         for t in range(1, NT):
@@ -121,9 +121,9 @@ def tile_list_gmu_silu_resL_kernel(
         def wplane(a, lo, hi):
             return wsc8[:, a * N + lo : a * N + hi]
 
-        def gather_tab_scales(h):
-            nc.vector.tensor_copy(gs[h][:], tabs[:].bitcast(U8).indirect(idx[:, cols(h)]))
-            nc.gpsimd.dma_start(out=gs1[h][0:112, :], in_=gs[h][16:128, :].bitcast(I32))
+        def gather_tab_scales():
+            nc.vector.tensor_copy(gs[:], tabs[:].bitcast(U8).indirect(idx[:]))
+            nc.scalar.dma_start(out=gs1[0:112, :], in_=gs[16:128, :].bitcast(I32))
 
         def gather_tab_words(h):
             nc.vector.tensor_copy(gw[h][:], tabw[:].bitcast(U32).indirect(idx[:, cols(h)]))
@@ -134,13 +134,13 @@ def tile_list_gmu_silu_resL_kernel(
         def gather_tab2_words(h):
             nc.vector.tensor_copy(gw2[h][:], tab2w[:].bitcast(U32).indirect(idx2[:, cols(h)]))
 
-        def gather_tab2_scales(h):
-            nc.vector.tensor_copy(gs2[h][:], tab2s[:].bitcast(U8).indirect(idx2[:, cols(h)]))
+        def gather_tab2_scales():
+            nc.vector.tensor_copy(gs2[:], tab2s[:].bitcast(U8).indirect(idx2[:]))
 
         def tab_plane(h, a, lo, hi):
             if a == 0:
-                return gs[h][:, lo:hi]
-            return gs1[h][:].bitcast(U8)[:, lo:hi]
+                return gs[:, h * H + lo : h * H + hi]
+            return gs1[:].bitcast(U8)[:, h * H + lo : h * H + hi]
 
         def tab_codes(h, a, lo, hi):
             return gsp[h][:, a, lo:hi].bitcast(FP4X4)
@@ -157,12 +157,12 @@ def tile_list_gmu_silu_resL_kernel(
                 )
             i = h * JT + s
             nc.scalar.activation(av[i][:], acc[:], ACT.Silu)
-            nc.gpsimd.tensor_tensor(dd[i][:], av[i][:], at[i][:], ALU.subtract)
+            nc.vector.tensor_tensor(dd[i][:], av[i][:], at[i][:], ALU.subtract)
 
         def ht_unit(h, s):
             acc = bank("mx", 4)
             nc.tensor.matmul_mx(
-                out=acc[:], lhsT=gw2[h][:, s * P : (s + 1) * P].bitcast(FP8X4), lhsT_scale=gs2[h][:, s * P : (s + 1) * P],
+                out=acc[:], lhsT=gw2[h][:, s * P : (s + 1) * P].bitcast(FP8X4), lhsT_scale=gs2[:, h * H + s * P : h * H + (s + 1) * P],
                 rhs=wtq[:].bitcast(FP8X4), rhs_scale=wts[:], start=True, stop=True,
             )
             i = h * JT + s
@@ -177,7 +177,7 @@ def tile_list_gmu_silu_resL_kernel(
                 )
             nc.tensor.matmul_mx(
                 out=acc[:], lhsT=ztw[:, t * 64 : (t + 1) * 64].bitcast(FP4X4), lhsT_scale=wplane(4, t * P, (t + 1) * P),
-                rhs=gw2[h][:].bitcast(FP8X4), rhs_scale=gs2[h][:], start=False, stop=True,
+                rhs=gw2[h][:].bitcast(FP8X4), rhs_scale=gs2[:, h * H : (h + 1) * H], start=False, stop=True,
             )
             nc.scalar.activation(th[h][t][:], acc[:], ACT.Tanh, bias=b_half[:, t : t + 1], scale=0.5)
 
@@ -189,7 +189,7 @@ def tile_list_gmu_silu_resL_kernel(
             nc.vector.scalar_tensor_tensor(ee[i][:], acc[:], 1.0, dd[i][:], ALU.add, ALU.mult)
 
         def gather_r(h, t):
-            nc.vector.tensor_copy(rg[h][t][:], r_win[t][:].indirect(idx[:, cols(h)]))
+            nc.vector.tensor_copy(rg[h][:, t, :], r_win[t][:].indirect(idx[:, cols(h)]))
 
         def out_unit(h, t):
             acc = bank("fin", 2)
@@ -201,8 +201,23 @@ def tile_list_gmu_silu_resL_kernel(
                         acc[:, s * P : (s + 1) * P], terms[u][:, t * P : (t + 1) * P], ident[:],
                         start=(u == 0), stop=(u == 2), is_transpose=True,
                     )
-            nc.vector.scalar_tensor_tensor(res[h][t][:], acc[:], 0.5, rg[h][t][:], ALU.mult, ALU.add)
-            nc.sync.dma_start(out=out[t * P : (t + 1) * P, h * H : (h + 1) * H], in_=res[h][t][:])
+            nc.vector.scalar_tensor_tensor(res[t][:], acc[:], 0.5, rg[h][:, t, :], ALU.mult, ALU.add)
+            nc.sync.dma_start(out=out[t * P : (t + 1) * P, h * H : (h + 1) * H], in_=res[t][:])
+
+        def out_unit_j(h, s):
+            acc = bank("fin", 2)
+            i = h * JT + s
+            terms = (at[i], at[i], ee[i])
+            for t in range(NT):
+                for u in range(3):
+                    nc.tensor.matmul(
+                        acc[:, t * P : (t + 1) * P], terms[u][:, t * P : (t + 1) * P], ident[:],
+                        start=(u == 0), stop=(u == 2), is_transpose=True,
+                    )
+            nc.vector.scalar_tensor_tensor(
+                res_j[s][:], acc[:].rearrange("p (t j) -> p t j", t=NT), 0.5, rg[h][:, :, s * P : (s + 1) * P], ALU.mult, ALU.add
+            )
+            nc.sync.dma_start(out=out.rearrange("(t p) j -> p t j", p=P)[:, :, i * P : (i + 1) * P], in_=res_j[s][:])
 
         def cast_wt(c):
             nc.scalar.copy(wt_bf[c][:], wt_raw[c][:].rearrange("p j n -> p n j"))
@@ -213,46 +228,34 @@ def tile_list_gmu_silu_resL_kernel(
 
         cast_wt(0)
         cast_wt(1)
-        gather_tab2_scales(0)
-        gather_tab2_scales(1)
+        gather_tab2_scales()
+        gather_tab_scales()
         gather_tab2_words(0)
-        gather_tab2_words(1)
         quantise_wt(0)
         quantise_wt(1)
-        for h in range(2):
-            for s in range(JT):
-                ht_unit(h, s)
-        gather_tab_scales(0)
-        gather_tab_scales(1)
+        for s in range(JT):
+            ht_unit(0, s)
         gather_tab_words(0)
         split(0)
-        for s in range(JT):
-            hv_unit(0, s)
+        gather_tab2_words(1)
         gather_tab_words(1)
         split(1)
+        for s in range(JT):
+            hv_unit(0, s)
         for t in range(NT):
             z_unit(0, t)
-        for s in range(JT):
-            hv_unit(1, s)
         gather_r(0, 0)
-        gather_r(1, 0)
-        for t in range(NT):
-            z_unit(1, t)
-        gather_r(0, 1)
-        gather_r(1, 1)
         for s in range(JT):
             e_unit(0, s)
-        gather_r(0, 2)
-        gather_r(1, 2)
-        out_unit(0, 0)
-        out_unit(0, 1)
+        for s in range(JT):
+            z_unit(1, s)
+            ht_unit(1, s)
+            hv_unit(1, s)
+            if s + 1 < NT:
+                gather_r(0, s + 1)
+            out_unit(0, s)
+            gather_r(1, s)
         for s in range(JT):
             e_unit(1, s)
-        out_unit(0, 2)
-        gather_r(0, 3)
-        out_unit(0, 3)
-        out_unit(1, 0)
-        gather_r(1, 3)
-        out_unit(1, 1)
-        out_unit(1, 2)
-        out_unit(1, 3)
+        for s in range(JT):
+            out_unit_j(1, s)

@@ -1,7 +1,6 @@
 from contextlib import ExitStack
 
 import concourse.mybir as mybir
-from concourse.masks import make_identity
 
 K, L, N, T, J = 1024, 512, 512, 2048, 1024
 FLOPS = 2 * N * J * (2 * K + 2 * L)
@@ -54,7 +53,6 @@ def tile_list_gmu_silu_resL_kernel(
         r_win = [sb(f"r_win{t}", [P, T], F32) for t in range(NT)]
         b_col = sb("b_col", [P, NT], F32)
         b_half = sb("b_half", [P, NT], F32)
-        ident = sb("ident", [P, P], F32)
         warm = sb("warm", [P, 8], F32)
         warm_o = sb("warm_o", [P, 8], F32)
 
@@ -64,14 +62,12 @@ def tile_list_gmu_silu_resL_kernel(
         gw = [sb(f"gw{h}", [P, H], U32) for h in range(2)]
         gsp = [sb(f"gsp{h}", [P, 2, H], U16) for h in range(2)]
         gw2 = [sb(f"gw2_{h}", [P, H], U32) for h in range(2)]
-        av = [sb(f"av{i}", [P, N], F32) for i in range(2 * JT)]
-        at = [sb(f"at{i}", [P, N], F32) for i in range(2 * JT)]
-        dd = [sb(f"dd{i}", [P, N], F32) for i in range(2 * JT)]
-        ee = [sb(f"ee{i}", [P, N], F32) for i in range(2 * JT)]
-        th = [[sb(f"th{h}_{t}", [P, H], F32) for t in range(NT)] for h in range(2)]
-        rg = [sb(f"rg{h}", [P, NT, H], F32) for h in range(2)]
-        res = [sb(f"res{t}", [P, H], F32) for t in range(NT)]
-        res_j = [sb(f"res_j{s}", [P, NT, P], F32) for s in range(JT)]
+        rg = [sb(f"rg{t}", [P, J], F32) for t in range(NT)]
+
+        def unit_tiles(name):
+            return {(h, t): sb(f"{name}{h}_{t}", [P, H], F32) for h in range(2) for t in range(NT)}
+
+        av, at, th, dd, uu, ee, res = [unit_tiles(x) for x in ("av", "at", "th", "dd", "uu", "ee", "res")]
 
         def cols(h):
             return slice(h * (H // 16), (h + 1) * (H // 16))
@@ -83,36 +79,36 @@ def tile_list_gmu_silu_resL_kernel(
         nc.scalar.activation(warm_o[:], warm[:], ACT.Silu)
         with nc.allow_non_contiguous_dma(reason="bias onto partitions"):
             nc.gpsimd.dma_start(out=b_col[:], in_=b.rearrange("(t p) -> p t", p=P))
-        make_identity(nc, ident[:])
 
         def load_scales(eng, dst, src, q):
             eng.dma_start(out=dst, in_=src[:, 4 * q : 4 * q + 4, :].rearrange("a r n -> r a n").bitcast(I32))
 
         wt_v = wt.rearrange("(p j) n -> p j n", j=4)
         tab_rows = tab_scales.rearrange("a (q r) t -> r q a t", r=4)
-        nc.sync.dma_start(idx2[:], offs2)
         for q in range(4):
             rows = tab2_scales[0, 4 * q : 4 * q + 4, :].bitcast(I32)
             nc.sync.dma_start(out=tab2s[32 * q : 32 * q + 32, :], in_=rows.unsqueeze(0).to_broadcast([8, 4, T // 4]))
+        nc.sync.dma_start(idx2[:], offs2)
         nc.sync.dma_start(idx[:], offs)
+        nc.sync.dma_start(out=tabw[:], in_=tab_words[0].rearrange("p t b -> p (t b)").bitcast(I32))
+        for q in range(4):
+            nc.sync.dma_start(out=wsc[32 * q : 32 * q + 4, 4, :], in_=zt_scales[0, 4 * q : 4 * q + 4, :].bitcast(I32))
+        nc.sync.dma_start(out=wvw[:], in_=wv_words.rearrange("a p n -> p a n").bitcast(I32))
+        nc.sync.dma_start(out=r_win[0][:], in_=rT[0:P, :])
+        nc.sync.dma_start(out=tab2w[:], in_=tab2_words[0].rearrange("p t b -> p (t b)").bitcast(I32))
         nc.sync.dma_start(out=wt_raw[0][:], in_=wt_v[:, :, 0 : N // 2])
         for r in range(4):
             nc.sync.dma_start(out=tabs[r:P:16, :], in_=tab_rows[r].bitcast(I32))
-        nc.sync.dma_start(out=tab2w[:], in_=tab2_words[0].rearrange("p t b -> p (t b)").bitcast(I32))
         nc.sync.dma_start(out=wt_raw[1][:], in_=wt_v[:, :, N // 2 : N])
-        nc.sync.dma_start(out=tabw[:], in_=tab_words[0].rearrange("p t b -> p (t b)").bitcast(I32))
         for q in range(4):
             load_scales(nc.sync, wsc[32 * q : 32 * q + 4, 0:2, :], wv_scales, q)
-        nc.sync.dma_start(out=wvw[:], in_=wv_words.rearrange("a p n -> p a n").bitcast(I32))
+        nc.sync.dma_start(out=ztw[:], in_=zt_words[0].bitcast(I32))
+        nc.sync.dma_start(out=r_win[1][:], in_=rT[P : 2 * P, :])
+        nc.sync.dma_start(out=r_win[2][:], in_=rT[2 * P : 3 * P, :])
         nc.sync.dma_start(out=zvw[:], in_=zv_words.rearrange("a p n -> p a n").bitcast(I32))
         for q in range(4):
             load_scales(nc.sync, wsc[32 * q : 32 * q + 4, 2:4, :], zv_scales, q)
-        nc.sync.dma_start(out=r_win[0][:], in_=rT[0:P, :])
-        nc.sync.dma_start(out=ztw[:], in_=zt_words[0].bitcast(I32))
-        for q in range(4):
-            nc.sync.dma_start(out=wsc[32 * q : 32 * q + 4, 4, :], in_=zt_scales[0, 4 * q : 4 * q + 4, :].bitcast(I32))
-        for t in range(1, NT):
-            nc.sync.dma_start(out=r_win[t][:], in_=rT[t * P : (t + 1) * P, :])
+        nc.sync.dma_start(out=r_win[3][:], in_=rT[3 * P : 4 * P, :])
 
         nc.scalar.activation(b_half[:], b_col[:], ACT.Copy, scale=0.5)
 
@@ -145,79 +141,49 @@ def tile_list_gmu_silu_resL_kernel(
         def tab_codes(h, a, lo, hi):
             return gsp[h][:, a, lo:hi].bitcast(FP4X4)
 
-        def bank(tag, bufs):
-            return psum.tile([P, 512], F32, name=tag, tag=tag, bufs=bufs)
+        def bank():
+            return psum.tile([P, 512], F32, name="mx", tag="mx", bufs=8)
 
-        def hv_unit(h, s):
-            acc = bank("mx", 4)
+        def tab_passes(acc, words, first_plane, h, t, stop):
             for a in range(2):
                 nc.tensor.matmul_mx(
-                    out=acc[:], lhsT=tab_codes(h, a, s * P, (s + 1) * P), lhsT_scale=tab_plane(h, a, s * P, (s + 1) * P),
-                    rhs=wvw[:, a, :].bitcast(FP4X4), rhs_scale=wplane(a, 0, N), start=(a == 0), stop=(a == 1),
+                    out=acc[:], lhsT=words[:, a, t * 64 : (t + 1) * 64].bitcast(FP4X4),
+                    lhsT_scale=wplane(first_plane + a, t * P, (t + 1) * P),
+                    rhs=tab_codes(h, a, 0, H), rhs_scale=tab_plane(h, a, 0, H), start=(a == 0), stop=(stop and a == 1),
                 )
-            i = h * JT + s
-            nc.scalar.activation(av[i][:], acc[:], ACT.Silu)
-            nc.vector.tensor_tensor(dd[i][:], av[i][:], at[i][:], ALU.subtract)
 
-        def ht_unit(h, s):
-            acc = bank("mx", 4)
+        def products(h, t):
+            u = (h, t)
+            acc = bank()
             nc.tensor.matmul_mx(
-                out=acc[:], lhsT=gw2[h][:, s * P : (s + 1) * P].bitcast(FP8X4), lhsT_scale=gs2[:, h * H + s * P : h * H + (s + 1) * P],
-                rhs=wtq[:].bitcast(FP8X4), rhs_scale=wts[:], start=True, stop=True,
+                out=acc[:], lhsT=wtq[:, t * P : (t + 1) * P].bitcast(FP8X4), lhsT_scale=wts[:, t * P : (t + 1) * P],
+                rhs=gw2[h][:].bitcast(FP8X4), rhs_scale=gs2[:, h * H : (h + 1) * H], start=True, stop=True,
             )
-            i = h * JT + s
-            nc.scalar.activation(at[i][:], acc[:], ACT.Silu)
-
-        def z_unit(h, t):
-            acc = bank("mx", 4)
-            for a in range(2):
-                nc.tensor.matmul_mx(
-                    out=acc[:], lhsT=zvw[:, a, t * 64 : (t + 1) * 64].bitcast(FP4X4), lhsT_scale=wplane(2 + a, t * P, (t + 1) * P),
-                    rhs=tab_codes(h, a, 0, H), rhs_scale=tab_plane(h, a, 0, H), start=(a == 0), stop=False,
-                )
+            nc.scalar.activation(at[u][:], acc[:], ACT.Silu)
+            acc = bank()
+            tab_passes(acc, wvw, 0, h, t, True)
+            nc.scalar.activation(av[u][:], acc[:], ACT.Silu)
+            nc.vector.tensor_tensor(dd[u][:], av[u][:], at[u][:], ALU.subtract)
+            acc = bank()
+            tab_passes(acc, zvw, 2, h, t, False)
             nc.tensor.matmul_mx(
                 out=acc[:], lhsT=ztw[:, t * 64 : (t + 1) * 64].bitcast(FP4X4), lhsT_scale=wplane(4, t * P, (t + 1) * P),
                 rhs=gw2[h][:].bitcast(FP8X4), rhs_scale=gs2[:, h * H : (h + 1) * H], start=False, stop=True,
             )
-            nc.scalar.activation(th[h][t][:], acc[:], ACT.Tanh, bias=b_half[:, t : t + 1], scale=0.5)
+            nc.scalar.activation(th[u][:], acc[:], ACT.Tanh, bias=b_half[:, t : t + 1], scale=0.5)
 
-        def e_unit(h, s):
-            acc = bank("tt", 2)
-            for t in range(NT):
-                nc.tensor.transpose(acc[:, t * P : (t + 1) * P], th[h][t][:, s * P : (s + 1) * P], ident[:])
-            i = h * JT + s
-            nc.vector.scalar_tensor_tensor(ee[i][:], acc[:], 1.0, dd[i][:], ALU.add, ALU.mult)
+        def gather_r(t):
+            nc.vector.tensor_copy(rg[t][:], r_win[t][:].indirect(idx[:]))
 
-        def gather_r(h, t):
-            nc.vector.tensor_copy(rg[h][:, t, :], r_win[t][:].indirect(idx[:, cols(h)]))
+        def mix(h, t):
+            u = (h, t)
+            nc.vector.tensor_tensor(uu[u][:], at[u][:], rg[t][:, h * H : (h + 1) * H], ALU.add)
+            nc.vector.scalar_tensor_tensor(ee[u][:], th[u][:], 1.0, dd[u][:], ALU.add, ALU.mult)
 
-        def out_unit(h, t):
-            acc = bank("fin", 2)
-            for s in range(JT):
-                i = h * JT + s
-                terms = (at[i], at[i], ee[i])
-                for u in range(3):
-                    nc.tensor.matmul(
-                        acc[:, s * P : (s + 1) * P], terms[u][:, t * P : (t + 1) * P], ident[:],
-                        start=(u == 0), stop=(u == 2), is_transpose=True,
-                    )
-            nc.vector.scalar_tensor_tensor(res[t][:], acc[:], 0.5, rg[h][:, t, :], ALU.mult, ALU.add)
-            nc.sync.dma_start(out=out[t * P : (t + 1) * P, h * H : (h + 1) * H], in_=res[t][:])
-
-        def out_unit_j(h, s):
-            acc = bank("fin", 2)
-            i = h * JT + s
-            terms = (at[i], at[i], ee[i])
-            for t in range(NT):
-                for u in range(3):
-                    nc.tensor.matmul(
-                        acc[:, t * P : (t + 1) * P], terms[u][:, t * P : (t + 1) * P], ident[:],
-                        start=(u == 0), stop=(u == 2), is_transpose=True,
-                    )
-            nc.vector.scalar_tensor_tensor(
-                res_j[s][:], acc[:].rearrange("p (t j) -> p t j", t=NT), 0.5, rg[h][:, :, s * P : (s + 1) * P], ALU.mult, ALU.add
-            )
-            nc.sync.dma_start(out=out.rearrange("(t p) j -> p t j", p=P)[:, :, i * P : (i + 1) * P], in_=res_j[s][:])
+        def finish(h, t):
+            u = (h, t)
+            nc.vector.scalar_tensor_tensor(res[u][:], ee[u][:], 0.5, uu[u][:], ALU.mult, ALU.add)
+            nc.sync.dma_start(out=out[t * P : (t + 1) * P, h * H : (h + 1) * H], in_=res[u][:])
 
         def cast_wt(c):
             nc.scalar.copy(wt_bf[c][:], wt_raw[c][:].rearrange("p j n -> p n j"))
@@ -230,32 +196,20 @@ def tile_list_gmu_silu_resL_kernel(
         cast_wt(1)
         gather_tab2_scales()
         gather_tab_scales()
+        gather_tab_words(0)
         gather_tab2_words(0)
+        split(0)
         quantise_wt(0)
         quantise_wt(1)
-        for s in range(JT):
-            ht_unit(0, s)
-        gather_tab_words(0)
-        split(0)
-        gather_tab2_words(1)
         gather_tab_words(1)
+        gather_tab2_words(1)
         split(1)
-        for s in range(JT):
-            hv_unit(0, s)
-        for t in range(NT):
-            z_unit(0, t)
-        gather_r(0, 0)
-        for s in range(JT):
-            e_unit(0, s)
-        for s in range(JT):
-            z_unit(1, s)
-            ht_unit(1, s)
-            hv_unit(1, s)
-            if s + 1 < NT:
-                gather_r(0, s + 1)
-            out_unit(0, s)
-            gather_r(1, s)
-        for s in range(JT):
-            e_unit(1, s)
-        for s in range(JT):
-            out_unit_j(1, s)
+        units = [(h, t) for h in range(2) for t in range(NT)]
+        for i, (h, t) in enumerate(units):
+            if h == 0:
+                gather_r(t)
+            products(h, t)
+            mix(h, t)
+            if i > 0:
+                finish(*units[i - 1])
+        finish(*units[-1])

@@ -1,6 +1,7 @@
 from contextlib import ExitStack
 
 import concourse.mybir as mybir
+from concourse.masks import make_identity
 
 K, L, N, T, J = 1024, 512, 512, 2048, 1024
 FLOPS = 2 * N * J * (2 * K + 2 * L)
@@ -51,7 +52,8 @@ def tile_list_gmu_silu_resL_kernel(
         wtq = sb("wtq", [P, N], U32)
         wts = sb("wts", [P, N], U8)
         r_win = [sb(f"r_win{t}", [P, T], F32) for t in range(NT)]
-        b_col = sb("b_col", [P, NT], F32)
+        b_rows = sb("b_rows", [P, P], F32)
+        ident = sb("ident", [P, P], F32)
         b_half = sb("b_half", [P, NT], F32)
         warm = sb("warm", [P, 8], F32)
         warm_o = sb("warm_o", [P, 8], F32)
@@ -77,40 +79,39 @@ def tile_list_gmu_silu_resL_kernel(
         nc.vector.memset(gs1[:], 0)
         nc.vector.memset(warm[:], 0.0)
         nc.scalar.activation(warm_o[:], warm[:], ACT.Silu)
-        with nc.allow_non_contiguous_dma(reason="bias onto partitions"):
-            nc.gpsimd.dma_start(out=b_col[:], in_=b.rearrange("(t p) -> p t", p=P))
+        nc.vector.memset(b_rows[:], 0.0)
+        make_identity(nc, ident[:])
 
         def load_scales(eng, dst, src, q):
             eng.dma_start(out=dst, in_=src[:, 4 * q : 4 * q + 4, :].rearrange("a r n -> r a n").bitcast(I32))
 
         wt_v = wt.rearrange("(p j) n -> p j n", j=4)
         tab_rows = tab_scales.rearrange("a (q r) t -> r q a t", r=4)
+        nc.sync.dma_start(idx[:], offs)
+        nc.sync.dma_start(idx2[:], offs2)
+        for r in range(4):
+            nc.sync.dma_start(out=tabs[r:P:16, :], in_=tab_rows[r].bitcast(I32))
         for q in range(4):
             rows = tab2_scales[0, 4 * q : 4 * q + 4, :].bitcast(I32)
             nc.sync.dma_start(out=tab2s[32 * q : 32 * q + 32, :], in_=rows.unsqueeze(0).to_broadcast([8, 4, T // 4]))
-        nc.sync.dma_start(idx2[:], offs2)
-        nc.sync.dma_start(idx[:], offs)
+        nc.sync.dma_start(out=tab2w[:], in_=tab2_words[0].rearrange("p t b -> p (t b)").bitcast(I32))
         nc.sync.dma_start(out=tabw[:], in_=tab_words[0].rearrange("p t b -> p (t b)").bitcast(I32))
         for q in range(4):
-            nc.sync.dma_start(out=wsc[32 * q : 32 * q + 4, 4, :], in_=zt_scales[0, 4 * q : 4 * q + 4, :].bitcast(I32))
-        nc.sync.dma_start(out=wvw[:], in_=wv_words.rearrange("a p n -> p a n").bitcast(I32))
-        nc.sync.dma_start(out=r_win[0][:], in_=rT[0:P, :])
-        nc.sync.dma_start(out=tab2w[:], in_=tab2_words[0].rearrange("p t b -> p (t b)").bitcast(I32))
-        nc.sync.dma_start(out=wt_raw[0][:], in_=wt_v[:, :, 0 : N // 2])
-        for r in range(4):
-            nc.sync.dma_start(out=tabs[r:P:16, :], in_=tab_rows[r].bitcast(I32))
-        nc.sync.dma_start(out=wt_raw[1][:], in_=wt_v[:, :, N // 2 : N])
-        for q in range(4):
             load_scales(nc.sync, wsc[32 * q : 32 * q + 4, 0:2, :], wv_scales, q)
-        nc.sync.dma_start(out=ztw[:], in_=zt_words[0].bitcast(I32))
-        nc.sync.dma_start(out=r_win[1][:], in_=rT[P : 2 * P, :])
-        nc.sync.dma_start(out=r_win[2][:], in_=rT[2 * P : 3 * P, :])
-        nc.sync.dma_start(out=zvw[:], in_=zv_words.rearrange("a p n -> p a n").bitcast(I32))
+        nc.sync.dma_start(out=wt_raw[0][:], in_=wt_v[:, :, 0 : N // 2])
+        nc.sync.dma_start(out=r_win[0][:], in_=rT[0 * P : 1 * P, :])
+        nc.sync.dma_start(out=wvw[:], in_=wv_words.rearrange("a p n -> p a n").bitcast(I32))
         for q in range(4):
             load_scales(nc.sync, wsc[32 * q : 32 * q + 4, 2:4, :], zv_scales, q)
+        nc.sync.dma_start(out=ztw[:], in_=zt_words[0].bitcast(I32))
+        nc.sync.dma_start(out=r_win[1][:], in_=rT[1 * P : 2 * P, :])
+        for q in range(4):
+            nc.sync.dma_start(out=wsc[32 * q : 32 * q + 4, 4, :], in_=zt_scales[0, 4 * q : 4 * q + 4, :].bitcast(I32))
+        nc.sync.dma_start(out=b_rows[0:NT, :], in_=b.rearrange("(t p) -> t p", p=P))
+        nc.sync.dma_start(out=zvw[:], in_=zv_words.rearrange("a p n -> p a n").bitcast(I32))
+        nc.sync.dma_start(out=wt_raw[1][:], in_=wt_v[:, :, N // 2 : N])
+        nc.sync.dma_start(out=r_win[2][:], in_=rT[2 * P : 3 * P, :])
         nc.sync.dma_start(out=r_win[3][:], in_=rT[3 * P : 4 * P, :])
-
-        nc.scalar.activation(b_half[:], b_col[:], ACT.Copy, scale=0.5)
 
         wsc8 = wsc[:].rearrange("p a n -> p (a n)").bitcast(U8)
 
@@ -141,8 +142,8 @@ def tile_list_gmu_silu_resL_kernel(
         def tab_codes(h, a, lo, hi):
             return gsp[h][:, a, lo:hi].bitcast(FP4X4)
 
-        def bank():
-            return psum.tile([P, 512], F32, name="mx", tag="mx", bufs=8)
+        def bank(tag="mx", bufs=4):
+            return psum.tile([P, 512], F32, name=tag, tag=tag, bufs=bufs)
 
         def tab_passes(acc, words, first_plane, h, t, stop):
             for a in range(2):
@@ -175,15 +176,34 @@ def tile_list_gmu_silu_resL_kernel(
         def gather_r(t):
             nc.vector.tensor_copy(rg[t][:], r_win[t][:].indirect(idx[:]))
 
-        def mix(h, t):
+        def mix(h, t, on_tensor):
             u = (h, t)
-            nc.vector.tensor_tensor(uu[u][:], at[u][:], rg[t][:, h * H : (h + 1) * H], ALU.add)
+            if on_tensor:
+                acc = bank("turned", 2)
+                for s in range(JT):
+                    c = slice(s * P, (s + 1) * P)
+                    nc.tensor.matmul(acc[:, c], at[u][:, c], ident[:], start=True, stop=False, is_transpose=True)
+                    nc.tensor.matmul(acc[:, c], rg[t][:, h * H + s * P : h * H + (s + 1) * P], ident[:], start=False, stop=True, is_transpose=True)
+                nc.scalar.copy(uu[u][:], acc[:])
+            else:
+                nc.vector.tensor_tensor(uu[u][:], at[u][:], rg[t][:, h * H : (h + 1) * H], ALU.add)
             nc.vector.scalar_tensor_tensor(ee[u][:], th[u][:], 1.0, dd[u][:], ALU.add, ALU.mult)
 
-        def finish(h, t):
+        def finish(h, t, on_tensor, is_last):
             u = (h, t)
-            nc.vector.scalar_tensor_tensor(res[u][:], ee[u][:], 0.5, uu[u][:], ALU.mult, ALU.add)
-            nc.sync.dma_start(out=out[t * P : (t + 1) * P, h * H : (h + 1) * H], in_=res[u][:])
+            if on_tensor:
+                acc = bank("back", 2)
+                for s in range(JT):
+                    c = slice(s * P, (s + 1) * P)
+                    nc.tensor.transpose(acc[:, c], uu[u][:, c], ident[:])
+                nc.vector.scalar_tensor_tensor(res[u][:], ee[u][:], 0.5, acc[:], ALU.mult, ALU.add)
+                nc.sync.dma_start(out=out[t * P : (t + 1) * P, h * H : (h + 1) * H], in_=res[u][:])
+            else:
+                w = H // 2 if is_last else H
+                for c0 in range(0, H, w):
+                    c = slice(c0, c0 + w)
+                    nc.vector.scalar_tensor_tensor(res[u][:, c], ee[u][:, c], 0.5, uu[u][:, c], ALU.mult, ALU.add)
+                    nc.sync.dma_start(out=out[t * P : (t + 1) * P, h * H + c0 : h * H + c0 + w], in_=res[u][:, c])
 
         def cast_wt(c):
             nc.scalar.copy(wt_bf[c][:], wt_raw[c][:].rearrange("p j n -> p n j"))
@@ -204,12 +224,16 @@ def tile_list_gmu_silu_resL_kernel(
         gather_tab_words(1)
         gather_tab2_words(1)
         split(1)
-        units = [(h, t) for h in range(2) for t in range(NT)]
+        b_turned = bank("turned", 2)
+        nc.tensor.transpose(b_turned[:, 0:P], b_rows[:], ident[:])
+        nc.scalar.activation(b_half[:], b_turned[:, 0:NT], ACT.Copy, scale=0.5)
+        units = [(h, t) for t in range(NT) for h in range(2)]
+        last = len(units) - 1
         for i, (h, t) in enumerate(units):
             if h == 0:
                 gather_r(t)
             products(h, t)
-            mix(h, t)
+            mix(h, t, i < 6)
             if i > 0:
-                finish(*units[i - 1])
-        finish(*units[-1])
+                finish(*units[i - 1], i - 1 < 6, False)
+        finish(*units[last], False, True)

@@ -49,8 +49,8 @@ def tile_list_gmu_silu_resL_kernel(
         ztw = sb("ztw", [P, N // 2], I32)
         wt_raw = [sb(f"wt_raw{c}", [P, 4, N // 2], F32) for c in range(2)]
         wt_bf = [sb(f"wt_bf{c}", [P, N // 2, 4], BF16) for c in range(2)]
-        wtq = sb("wtq", [P, N], U32)
-        wts = sb("wts", [P, N], U8)
+        wtq = [sb(f"wtq{c}", [P, N // 2], U32) for c in range(2)]
+        wts = [sb(f"wts{c}", [P, N // 2], U8) for c in range(2)]
         r_win = [sb(f"r_win{t}", [P, T], F32) for t in range(NT)]
         b_rows = sb("b_rows", [P, P], F32)
         ident = sb("ident", [P, P], F32)
@@ -61,20 +61,17 @@ def tile_list_gmu_silu_resL_kernel(
         gs = sb("gs", [P, J], U8)
         gs1 = sb("gs1", [P, J // 4], I32)
         gs2 = sb("gs2", [P, J], U8)
-        gw = [sb(f"gw{h}", [P, H], U32) for h in range(2)]
-        gsp = [sb(f"gsp{h}", [P, 2, H], U16) for h in range(2)]
-        gw2 = [sb(f"gw2_{h}", [P, H], U32) for h in range(2)]
-        rg = [sb(f"rg{t}", [P, J], F32) for t in range(NT)]
+        gw = sb("gw", [P, J], U32)
+        gsp = sb("gsp", [P, 2, J], U16)
+        gw2 = sb("gw2", [P, J], U32)
 
-        def unit_tiles(name):
-            return {(h, t): sb(f"{name}{h}_{t}", [P, H], F32) for h in range(2) for t in range(NT)}
+        def row_tiles(name):
+            return [sb(f"{name}{t}", [P, J], F32) for t in range(NT)]
 
-        av, at, th, dd, uu, ee, res = [unit_tiles(x) for x in ("av", "at", "th", "dd", "uu", "ee", "res")]
+        av, at, th, uu, res = [row_tiles(x) for x in ("av", "at", "th", "uu", "res")]
 
-        def cols(h):
-            return slice(h * (H // 16), (h + 1) * (H // 16))
-
-        nc.vector.memset(tabs[:], 0)
+        nc.gpsimd.memset(tabs[:], 0)
+        nc.vector.memset(tab2s[:], 0)
         nc.vector.memset(wsc[:], 0)
         nc.vector.memset(gs1[:], 0)
         nc.vector.memset(warm[:], 0.0)
@@ -82,8 +79,13 @@ def tile_list_gmu_silu_resL_kernel(
         nc.vector.memset(b_rows[:], 0.0)
         make_identity(nc, ident[:])
 
-        def load_scales(eng, dst, src, q):
-            eng.dma_start(out=dst, in_=src[:, 4 * q : 4 * q + 4, :].rearrange("a r n -> r a n").bitcast(I32))
+        def load_scales(first, count, src):
+            for q in range(4):
+                rows = src[:, 4 * q : 4 * q + 4, :].rearrange("a r n -> r a n").bitcast(I32)
+                nc.sync.dma_start(out=wsc[32 * q : 32 * q + 4, first : first + count, :], in_=rows)
+
+        def load_r(t):
+            nc.sync.dma_start(out=r_win[t][:], in_=rT[t * P : (t + 1) * P, :])
 
         wt_v = wt.rearrange("(p j) n -> p j n", j=4)
         tab_rows = tab_scales.rearrange("a (q r) t -> r q a t", r=4)
@@ -91,149 +93,105 @@ def tile_list_gmu_silu_resL_kernel(
         nc.sync.dma_start(idx2[:], offs2)
         for r in range(4):
             nc.sync.dma_start(out=tabs[r:P:16, :], in_=tab_rows[r].bitcast(I32))
-        for q in range(4):
-            rows = tab2_scales[0, 4 * q : 4 * q + 4, :].bitcast(I32)
-            nc.sync.dma_start(out=tab2s[32 * q : 32 * q + 32, :], in_=rows.unsqueeze(0).to_broadcast([8, 4, T // 4]))
-        nc.sync.dma_start(out=tab2w[:], in_=tab2_words[0].rearrange("p t b -> p (t b)").bitcast(I32))
         nc.sync.dma_start(out=tabw[:], in_=tab_words[0].rearrange("p t b -> p (t b)").bitcast(I32))
-        for q in range(4):
-            load_scales(nc.sync, wsc[32 * q : 32 * q + 4, 0:2, :], wv_scales, q)
+        nc.sync.dma_start(out=tab2w[:], in_=tab2_words[0].rearrange("p t b -> p (t b)").bitcast(I32))
         nc.sync.dma_start(out=wt_raw[0][:], in_=wt_v[:, :, 0 : N // 2])
-        nc.sync.dma_start(out=r_win[0][:], in_=rT[0 * P : 1 * P, :])
         nc.sync.dma_start(out=wvw[:], in_=wv_words.rearrange("a p n -> p a n").bitcast(I32))
+        load_scales(0, 2, wv_scales)
+        load_r(0)
         for q in range(4):
-            load_scales(nc.sync, wsc[32 * q : 32 * q + 4, 2:4, :], zv_scales, q)
-        nc.sync.dma_start(out=ztw[:], in_=zt_words[0].bitcast(I32))
-        nc.sync.dma_start(out=r_win[1][:], in_=rT[1 * P : 2 * P, :])
-        for q in range(4):
-            nc.sync.dma_start(out=wsc[32 * q : 32 * q + 4, 4, :], in_=zt_scales[0, 4 * q : 4 * q + 4, :].bitcast(I32))
-        nc.sync.dma_start(out=b_rows[0:NT, :], in_=b.rearrange("(t p) -> t p", p=P))
+            nc.sync.dma_start(out=tab2s[32 * q : 32 * q + 4, :], in_=tab2_scales[0, 4 * q : 4 * q + 4, :].bitcast(I32))
         nc.sync.dma_start(out=zvw[:], in_=zv_words.rearrange("a p n -> p a n").bitcast(I32))
+        load_scales(2, 2, zv_scales)
+        nc.sync.dma_start(out=ztw[:], in_=zt_words[0].bitcast(I32))
+        load_scales(4, 1, zt_scales)
+        nc.sync.dma_start(out=b_rows[0:NT, :], in_=b.rearrange("(t p) -> t p", p=P))
         nc.sync.dma_start(out=wt_raw[1][:], in_=wt_v[:, :, N // 2 : N])
-        nc.sync.dma_start(out=r_win[2][:], in_=rT[2 * P : 3 * P, :])
-        nc.sync.dma_start(out=r_win[3][:], in_=rT[3 * P : 4 * P, :])
+        load_r(1)
+        load_r(2)
+        load_r(3)
 
         wsc8 = wsc[:].rearrange("p a n -> p (a n)").bitcast(U8)
 
-        def wplane(a, lo, hi):
-            return wsc8[:, a * N + lo : a * N + hi]
+        def wplane(a, t):
+            return wsc8[:, a * N + t * P : a * N + (t + 1) * P]
 
-        def gather_tab_scales():
-            nc.vector.tensor_copy(gs[:], tabs[:].bitcast(U8).indirect(idx[:]))
-            nc.scalar.dma_start(out=gs1[0:112, :], in_=gs[16:128, :].bitcast(I32))
+        def half(h):
+            return slice(h * H, (h + 1) * H)
 
-        def gather_tab_words(h):
-            nc.vector.tensor_copy(gw[h][:], tabw[:].bitcast(U32).indirect(idx[:, cols(h)]))
+        def tab_plane(h, a):
+            return gs[:, half(h)] if a == 0 else gs1[:].bitcast(U8)[:, half(h)]
 
-        def split(h):
-            nc.vector.tensor_copy(gsp[h][:], gw[h][:].bitcast(U16).rearrange("p (t d) -> p d t", d=2))
-
-        def gather_tab2_words(h):
-            nc.vector.tensor_copy(gw2[h][:], tab2w[:].bitcast(U32).indirect(idx2[:, cols(h)]))
-
-        def gather_tab2_scales():
-            nc.vector.tensor_copy(gs2[:], tab2s[:].bitcast(U8).indirect(idx2[:]))
-
-        def tab_plane(h, a, lo, hi):
-            if a == 0:
-                return gs[:, h * H + lo : h * H + hi]
-            return gs1[:].bitcast(U8)[:, h * H + lo : h * H + hi]
-
-        def tab_codes(h, a, lo, hi):
-            return gsp[h][:, a, lo:hi].bitcast(FP4X4)
-
-        def bank(tag="mx", bufs=4):
-            return psum.tile([P, 512], F32, name=tag, tag=tag, bufs=bufs)
+        def bank():
+            return psum.tile([P, H], F32, name="acc", tag="acc", bufs=8)
 
         def tab_passes(acc, words, first_plane, h, t, stop):
             for a in range(2):
                 nc.tensor.matmul_mx(
                     out=acc[:], lhsT=words[:, a, t * 64 : (t + 1) * 64].bitcast(FP4X4),
-                    lhsT_scale=wplane(first_plane + a, t * P, (t + 1) * P),
-                    rhs=tab_codes(h, a, 0, H), rhs_scale=tab_plane(h, a, 0, H), start=(a == 0), stop=(stop and a == 1),
+                    lhsT_scale=wplane(first_plane + a, t),
+                    rhs=gsp[:, a, half(h)].bitcast(FP4X4), rhs_scale=tab_plane(h, a), start=(a == 0), stop=(stop and a == 1),
                 )
 
-        def products(h, t):
-            u = (h, t)
-            acc = bank()
-            nc.tensor.matmul_mx(
-                out=acc[:], lhsT=wtq[:, t * P : (t + 1) * P].bitcast(FP8X4), lhsT_scale=wts[:, t * P : (t + 1) * P],
-                rhs=gw2[h][:].bitcast(FP8X4), rhs_scale=gs2[:, h * H : (h + 1) * H], start=True, stop=True,
-            )
-            nc.scalar.activation(at[u][:], acc[:], ACT.Silu)
+        def product_v(h, t):
             acc = bank()
             tab_passes(acc, wvw, 0, h, t, True)
-            nc.scalar.activation(av[u][:], acc[:], ACT.Silu)
-            nc.vector.tensor_tensor(dd[u][:], av[u][:], at[u][:], ALU.subtract)
+            nc.scalar.activation(av[t][:, half(h)], acc[:], ACT.Silu)
+
+        def product_t(h, t):
+            acc = bank()
+            c = slice((t % 2) * P, (t % 2 + 1) * P)
+            nc.tensor.matmul_mx(
+                out=acc[:], lhsT=wtq[t // 2][:, c].bitcast(FP8X4), lhsT_scale=wts[t // 2][:, c],
+                rhs=gw2[:, half(h)].bitcast(FP8X4), rhs_scale=gs2[:, half(h)], start=True, stop=True,
+            )
+            nc.scalar.activation(at[t][:, half(h)], acc[:], ACT.Silu)
+
+        def product_z(h, t):
             acc = bank()
             tab_passes(acc, zvw, 2, h, t, False)
             nc.tensor.matmul_mx(
-                out=acc[:], lhsT=ztw[:, t * 64 : (t + 1) * 64].bitcast(FP4X4), lhsT_scale=wplane(4, t * P, (t + 1) * P),
-                rhs=gw2[h][:].bitcast(FP8X4), rhs_scale=gs2[:, h * H : (h + 1) * H], start=False, stop=True,
+                out=acc[:], lhsT=ztw[:, t * 64 : (t + 1) * 64].bitcast(FP4X4), lhsT_scale=wplane(4, t),
+                rhs=gw2[:, half(h)].bitcast(FP8X4), rhs_scale=gs2[:, half(h)], start=False, stop=True,
             )
-            nc.scalar.activation(th[u][:], acc[:], ACT.Tanh, bias=b_half[:, t : t + 1], scale=0.5)
-
-        def gather_r(t):
-            nc.vector.tensor_copy(rg[t][:], r_win[t][:].indirect(idx[:]))
-
-        def mix(h, t, on_tensor):
-            u = (h, t)
-            if on_tensor:
-                acc = bank("turned", 2)
-                for s in range(JT):
-                    c = slice(s * P, (s + 1) * P)
-                    nc.tensor.matmul(acc[:, c], at[u][:, c], ident[:], start=True, stop=False, is_transpose=True)
-                    nc.tensor.matmul(acc[:, c], rg[t][:, h * H + s * P : h * H + (s + 1) * P], ident[:], start=False, stop=True, is_transpose=True)
-                nc.scalar.copy(uu[u][:], acc[:])
-            else:
-                nc.vector.tensor_tensor(uu[u][:], at[u][:], rg[t][:, h * H : (h + 1) * H], ALU.add)
-            nc.vector.scalar_tensor_tensor(ee[u][:], th[u][:], 1.0, dd[u][:], ALU.add, ALU.mult)
-
-        def finish(h, t, on_tensor, is_last):
-            u = (h, t)
-            if on_tensor:
-                acc = bank("back", 2)
-                for s in range(JT):
-                    c = slice(s * P, (s + 1) * P)
-                    nc.tensor.transpose(acc[:, c], uu[u][:, c], ident[:])
-                nc.vector.scalar_tensor_tensor(res[u][:], ee[u][:], 0.5, acc[:], ALU.mult, ALU.add)
-                nc.sync.dma_start(out=out[t * P : (t + 1) * P, h * H : (h + 1) * H], in_=res[u][:])
-            else:
-                w = H // 2 if is_last else H
-                for c0 in range(0, H, w):
-                    c = slice(c0, c0 + w)
-                    nc.vector.scalar_tensor_tensor(res[u][:, c], ee[u][:, c], 0.5, uu[u][:, c], ALU.mult, ALU.add)
-                    nc.sync.dma_start(out=out[t * P : (t + 1) * P, h * H + c0 : h * H + c0 + w], in_=res[u][:, c])
+            nc.scalar.activation(th[t][:, half(h)], acc[:], ACT.Tanh, bias=b_half[:, t : t + 1], scale=0.5)
 
         def cast_wt(c):
             nc.scalar.copy(wt_bf[c][:], wt_raw[c][:].rearrange("p j n -> p n j"))
 
         def quantise_wt(c):
-            lo, hi = c * (N // 2), (c + 1) * (N // 2)
-            nc.vector.quantize_mx(out=wtq[:, lo:hi].bitcast(FP8X4), scales=wts[:, lo:hi], in_=wt_bf[c][:].rearrange("p n j -> p (n j)"))
+            nc.vector.quantize_mx(out=wtq[c][:].bitcast(FP8X4), scales=wts[c][:], in_=wt_bf[c][:].rearrange("p n j -> p (n j)"))
 
+        nc.vector.tensor_copy(gs[:], tabs[:].bitcast(U8).indirect(idx[:]))
+        nc.scalar.dma_start(out=gs1[0:112, :], in_=gs[16:128, :].bitcast(I32))
+        nc.vector.tensor_copy(gw[:], tabw[:].bitcast(U32).indirect(idx[:]))
+        nc.vector.tensor_copy(gsp[:], gw[:].bitcast(U16).rearrange("p (t d) -> p d t", d=2))
+        nc.vector.tensor_copy(gw2[:], tab2w[:].bitcast(U32).indirect(idx2[:]))
+        nc.vector.tensor_copy(gs2[:], tab2s[:].bitcast(U8).indirect(idx2[:]))
         cast_wt(0)
-        cast_wt(1)
-        gather_tab2_scales()
-        gather_tab_scales()
-        gather_tab_words(0)
-        gather_tab2_words(0)
-        split(0)
         quantise_wt(0)
-        quantise_wt(1)
-        gather_tab_words(1)
-        gather_tab2_words(1)
-        split(1)
-        b_turned = bank("turned", 2)
+        for t in range(NT):
+            for h in range(2):
+                product_v(h, t)
+        b_turned = bank()
         nc.tensor.transpose(b_turned[:, 0:P], b_rows[:], ident[:])
         nc.scalar.activation(b_half[:], b_turned[:, 0:NT], ACT.Copy, scale=0.5)
-        units = [(h, t) for t in range(NT) for h in range(2)]
-        last = len(units) - 1
-        for i, (h, t) in enumerate(units):
-            if h == 0:
-                gather_r(t)
-            products(h, t)
-            mix(h, t, i < 6)
-            if i > 0:
-                finish(*units[i - 1], i - 1 < 6, False)
-        finish(*units[last], False, True)
+
+        def finish(t, pieces):
+            nc.vector.tensor_tensor(uu[t][:], r_win[t][:].indirect(idx[:]), av[t][:], ALU.add)
+            for h in range(2):
+                nc.vector.tensor_tensor(av[t][:, half(h)], av[t][:, half(h)], at[t][:, half(h)], ALU.subtract)
+            for h in range(2):
+                nc.vector.scalar_tensor_tensor(th[t][:, half(h)], th[t][:, half(h)], -1.0, av[t][:, half(h)], ALU.add, ALU.mult)
+            for c in pieces:
+                nc.vector.scalar_tensor_tensor(res[t][:, c], th[t][:, c], 0.5, uu[t][:, c], ALU.mult, ALU.add)
+                nc.sync.dma_start(out=out[t * P : (t + 1) * P, c], in_=res[t][:, c])
+
+        for t in range(NT):
+            if t == 1:
+                cast_wt(1)
+                quantise_wt(1)
+            for h in range(2):
+                product_t(h, t)
+                product_z(h, t)
+            finish(t, [half(0), half(1)] if t < NT - 1 else [half(0), slice(512, 768), slice(768, J)])

@@ -69,6 +69,7 @@ def tile_list_gmu_silu_resL_kernel(
             return [sb(f"{name}{t}", [P, J], F32) for t in range(NT)]
 
         av, at, th, uu, res = [row_tiles(x) for x in ("av", "at", "th", "uu", "res")]
+        turned = [sb(f"turned{t}", [P, J], F32) for t in range(NT - 1)]
 
         nc.gpsimd.memset(tabs[:], 0)
         nc.vector.memset(tab2s[:], 0)
@@ -95,19 +96,21 @@ def tile_list_gmu_silu_resL_kernel(
             nc.sync.dma_start(out=tabs[r:P:16, :], in_=tab_rows[r].bitcast(I32))
         nc.sync.dma_start(out=tabw[:], in_=tab_words[0].rearrange("p t b -> p (t b)").bitcast(I32))
         nc.sync.dma_start(out=tab2w[:], in_=tab2_words[0].rearrange("p t b -> p (t b)").bitcast(I32))
-        nc.sync.dma_start(out=wt_raw[0][:], in_=wt_v[:, :, 0 : N // 2])
-        nc.sync.dma_start(out=wvw[:], in_=wv_words.rearrange("a p n -> p a n").bitcast(I32))
-        load_scales(0, 2, wv_scales)
-        load_r(0)
         for q in range(4):
             nc.sync.dma_start(out=tab2s[32 * q : 32 * q + 4, :], in_=tab2_scales[0, 4 * q : 4 * q + 4, :].bitcast(I32))
+        nc.vector.tensor_copy(gs[:], tabs[:].bitcast(U8).indirect(idx[:]))
+        nc.sync.dma_start(out=gs1[0:112, :], in_=gs[16:128, :].bitcast(I32))
+        nc.sync.dma_start(out=wvw[:], in_=wv_words.rearrange("a p n -> p a n").bitcast(I32))
+        nc.sync.dma_start(out=wt_raw[0][:], in_=wt_v[:, :, 0 : N // 2])
+        load_scales(0, 2, wv_scales)
+        nc.sync.dma_start(out=wt_raw[1][:], in_=wt_v[:, :, N // 2 : N])
+        load_r(0)
+        load_r(1)
+        nc.sync.dma_start(out=b_rows[0:NT, :], in_=b.rearrange("(t p) -> t p", p=P))
         nc.sync.dma_start(out=zvw[:], in_=zv_words.rearrange("a p n -> p a n").bitcast(I32))
         load_scales(2, 2, zv_scales)
         nc.sync.dma_start(out=ztw[:], in_=zt_words[0].bitcast(I32))
         load_scales(4, 1, zt_scales)
-        nc.sync.dma_start(out=b_rows[0:NT, :], in_=b.rearrange("(t p) -> t p", p=P))
-        nc.sync.dma_start(out=wt_raw[1][:], in_=wt_v[:, :, N // 2 : N])
-        load_r(1)
         load_r(2)
         load_r(3)
 
@@ -162,14 +165,13 @@ def tile_list_gmu_silu_resL_kernel(
         def quantise_wt(c):
             nc.vector.quantize_mx(out=wtq[c][:].bitcast(FP8X4), scales=wts[c][:], in_=wt_bf[c][:].rearrange("p n j -> p (n j)"))
 
-        nc.vector.tensor_copy(gs[:], tabs[:].bitcast(U8).indirect(idx[:]))
-        nc.scalar.dma_start(out=gs1[0:112, :], in_=gs[16:128, :].bitcast(I32))
         nc.vector.tensor_copy(gw[:], tabw[:].bitcast(U32).indirect(idx[:]))
         nc.vector.tensor_copy(gsp[:], gw[:].bitcast(U16).rearrange("p (t d) -> p d t", d=2))
         nc.vector.tensor_copy(gw2[:], tab2w[:].bitcast(U32).indirect(idx2[:]))
         nc.vector.tensor_copy(gs2[:], tab2s[:].bitcast(U8).indirect(idx2[:]))
-        cast_wt(0)
-        quantise_wt(0)
+        for c in range(2):
+            cast_wt(c)
+            quantise_wt(c)
         for t in range(NT):
             for h in range(2):
                 product_v(h, t)
@@ -177,21 +179,43 @@ def tile_list_gmu_silu_resL_kernel(
         nc.tensor.transpose(b_turned[:, 0:P], b_rows[:], ident[:])
         nc.scalar.activation(b_half[:], b_turned[:, 0:NT], ACT.Copy, scale=0.5)
 
-        def finish(t, pieces):
+        def mix(t):
             nc.vector.tensor_tensor(uu[t][:], r_win[t][:].indirect(idx[:]), av[t][:], ALU.add)
             for h in range(2):
                 nc.vector.tensor_tensor(av[t][:, half(h)], av[t][:, half(h)], at[t][:, half(h)], ALU.subtract)
             for h in range(2):
                 nc.vector.scalar_tensor_tensor(th[t][:, half(h)], th[t][:, half(h)], -1.0, av[t][:, half(h)], ALU.add, ALU.mult)
+
+        def finish_on_vector(t, pieces):
             for c in pieces:
                 nc.vector.scalar_tensor_tensor(res[t][:, c], th[t][:, c], 0.5, uu[t][:, c], ALU.mult, ALU.add)
                 nc.sync.dma_start(out=out[t * P : (t + 1) * P, c], in_=res[t][:, c])
 
-        for t in range(NT):
-            if t == 1:
-                cast_wt(1)
-                quantise_wt(1)
+        def finish_on_tensor(t):
             for h in range(2):
-                product_t(h, t)
-                product_z(h, t)
-            finish(t, [half(0), half(1)] if t < NT - 1 else [half(0), slice(512, 768), slice(768, J)])
+                acc = bank()
+                for s in range(JT):
+                    c = slice(s * P, (s + 1) * P)
+                    j = slice(h * H + s * P, h * H + (s + 1) * P)
+                    nc.tensor.matmul(acc[:, c], uu[t][:, j], ident[:], start=True, stop=False, is_transpose=True)
+                    nc.tensor.matmul(acc[:, c], uu[t][:, j], ident[:], start=False, stop=False, is_transpose=True)
+                    nc.tensor.matmul(acc[:, c], th[t][:, j], ident[:], start=False, stop=True, is_transpose=True)
+                nc.scalar.activation(turned[t][:, half(h)], acc[:], ACT.Copy, scale=0.5)
+            for h in range(2):
+                acc = bank()
+                for s in range(JT):
+                    j = slice(h * H + s * P, h * H + (s + 1) * P)
+                    nc.tensor.transpose(acc[:, s * P : (s + 1) * P], turned[t][:, j], ident[:])
+                nc.scalar.copy(res[t][:, half(h)], acc[:])
+                nc.sync.dma_start(out=out[t * P : (t + 1) * P, half(h)], in_=res[t][:, half(h)])
+
+        for pair in range(NT // 2):
+            for product in (product_t, product_z):
+                for t in (2 * pair, 2 * pair + 1):
+                    for h in range(2):
+                        product(h, t)
+        for t in range(NT):
+            mix(t)
+        for t in range(NT - 1):
+            finish_on_tensor(t)
+        finish_on_vector(NT - 1, [half(0), slice(512, 768), slice(768, J)])

@@ -105,12 +105,12 @@ def tile_list_gmu_silu_resL_kernel(
         load_scales(0, 2, wv_scales)
         nc.sync.dma_start(out=wt_raw[1][:], in_=wt_v[:, :, N // 2 : N])
         load_r(0)
-        load_r(1)
-        nc.sync.dma_start(out=b_rows[0:NT, :], in_=b.rearrange("(t p) -> t p", p=P))
-        nc.sync.dma_start(out=zvw[:], in_=zv_words.rearrange("a p n -> p a n").bitcast(I32))
         load_scales(2, 2, zv_scales)
+        nc.sync.dma_start(out=zvw[:], in_=zv_words.rearrange("a p n -> p a n").bitcast(I32))
         nc.sync.dma_start(out=ztw[:], in_=zt_words[0].bitcast(I32))
         load_scales(4, 1, zt_scales)
+        nc.sync.dma_start(out=b_rows[0:NT, :], in_=b.rearrange("(t p) -> t p", p=P))
+        load_r(1)
         load_r(2)
         load_r(3)
 
@@ -172,12 +172,10 @@ def tile_list_gmu_silu_resL_kernel(
         for c in range(2):
             cast_wt(c)
             quantise_wt(c)
-        for t in range(NT):
+
+        def both(step, t):
             for h in range(2):
-                product_v(h, t)
-        b_turned = bank()
-        nc.tensor.transpose(b_turned[:, 0:P], b_rows[:], ident[:])
-        nc.scalar.activation(b_half[:], b_turned[:, 0:NT], ACT.Copy, scale=0.5)
+                step(h, t)
 
         def mix(t):
             nc.vector.tensor_tensor(uu[t][:], r_win[t][:].indirect(idx[:]), av[t][:], ALU.add)
@@ -186,36 +184,49 @@ def tile_list_gmu_silu_resL_kernel(
             for h in range(2):
                 nc.vector.scalar_tensor_tensor(th[t][:, half(h)], th[t][:, half(h)], -1.0, av[t][:, half(h)], ALU.add, ALU.mult)
 
-        def finish_on_vector(t, pieces):
-            for c in pieces:
-                nc.vector.scalar_tensor_tensor(res[t][:, c], th[t][:, c], 0.5, uu[t][:, c], ALU.mult, ALU.add)
-                nc.sync.dma_start(out=out[t * P : (t + 1) * P, c], in_=res[t][:, c])
+        def finish_on_vector(t, c):
+            nc.vector.scalar_tensor_tensor(res[t][:, c], th[t][:, c], 0.5, uu[t][:, c], ALU.mult, ALU.add)
+            nc.sync.dma_start(out=out[t * P : (t + 1) * P, c], in_=res[t][:, c])
 
-        def finish_on_tensor(t):
-            for h in range(2):
-                acc = bank()
-                for s in range(JT):
-                    c = slice(s * P, (s + 1) * P)
-                    j = slice(h * H + s * P, h * H + (s + 1) * P)
-                    nc.tensor.matmul(acc[:, c], uu[t][:, j], ident[:], start=True, stop=False, is_transpose=True)
-                    nc.tensor.matmul(acc[:, c], uu[t][:, j], ident[:], start=False, stop=False, is_transpose=True)
-                    nc.tensor.matmul(acc[:, c], th[t][:, j], ident[:], start=False, stop=True, is_transpose=True)
-                nc.scalar.activation(turned[t][:, half(h)], acc[:], ACT.Copy, scale=0.5)
-            for h in range(2):
-                acc = bank()
-                for s in range(JT):
-                    j = slice(h * H + s * P, h * H + (s + 1) * P)
-                    nc.tensor.transpose(acc[:, s * P : (s + 1) * P], turned[t][:, j], ident[:])
-                nc.scalar.copy(res[t][:, half(h)], acc[:])
-                nc.sync.dma_start(out=out[t * P : (t + 1) * P, half(h)], in_=res[t][:, half(h)])
+        def sum_turned(h, t):
+            acc = bank()
+            for s in range(JT):
+                c = slice(s * P, (s + 1) * P)
+                j = slice(h * H + s * P, h * H + (s + 1) * P)
+                nc.tensor.matmul(acc[:, c], uu[t][:, j], ident[:], start=True, stop=False, is_transpose=True)
+                nc.tensor.matmul(acc[:, c], uu[t][:, j], ident[:], start=False, stop=False, is_transpose=True)
+                nc.tensor.matmul(acc[:, c], th[t][:, j], ident[:], start=False, stop=True, is_transpose=True)
+            nc.scalar.activation(turned[t][:, half(h)], acc[:], ACT.Copy, scale=0.5)
 
-        for pair in range(NT // 2):
-            for product in (product_t, product_z):
-                for t in (2 * pair, 2 * pair + 1):
-                    for h in range(2):
-                        product(h, t)
-        for t in range(NT):
-            mix(t)
+        def turn_back(h, t):
+            acc = bank()
+            for s in range(JT):
+                j = slice(h * H + s * P, h * H + (s + 1) * P)
+                nc.tensor.transpose(acc[:, s * P : (s + 1) * P], turned[t][:, j], ident[:])
+            nc.scalar.copy(res[t][:, half(h)], acc[:])
+            nc.sync.dma_start(out=out[t * P : (t + 1) * P, half(h)], in_=res[t][:, half(h)])
+
         for t in range(NT - 1):
-            finish_on_tensor(t)
-        finish_on_vector(NT - 1, [half(0), slice(512, 768), slice(768, J)])
+            both(product_v, t)
+        both(product_t, 0)
+        b_turned = bank()
+        nc.tensor.transpose(b_turned[:, 0:P], b_rows[:], ident[:])
+        nc.scalar.activation(b_half[:], b_turned[:, 0:NT], ACT.Copy, scale=0.5)
+        both(product_z, 0)
+        mix(0)
+        both(product_v, NT - 1)
+        both(product_t, 1)
+        both(product_z, 1)
+        mix(1)
+        for t in range(2):
+            both(sum_turned, t)
+            both(product_t, t + 2)
+            both(turn_back, t)
+            both(product_z, t + 2)
+            mix(t + 2)
+            if t == 0:
+                finish_on_vector(2, half(1))
+        sum_turned(0, 2)
+        turn_back(0, 2)
+        for c in (half(0), slice(512, 768), slice(768, J)):
+            finish_on_vector(NT - 1, c)

@@ -40,17 +40,16 @@ def tile_list_gmu_silu_resL_kernel(
         idx2 = lists.tile([P, J // 16], U16, name="idx2")
 
         tabs = sb("tabs", [P, T // 4], I32)
-        tab2s = sb("tab2s", [P, T // 4], I32)
+        tab2s = keep.tile([P, T // 4], I32, name="tab2s", tag="tab2s_wtq", align_bytes=64)
         wsc = sb("wsc", [P, 5, N // 4], I32)
         tabw = sb("tabw", [P, T], I32)
         tab2w = sb("tab2w", [P, T], I32)
         wvw = sb("wvw", [P, 2, N // 2], I32)
         zvw = sb("zvw", [P, 2, N // 2], I32)
         ztw = sb("ztw", [P, N // 2], I32)
-        wt_raw = [sb(f"wt_raw{c}", [P, 4, N // 2], F32) for c in range(2)]
-        wt_bf = [sb(f"wt_bf{c}", [P, N // 2, 4], BF16) for c in range(2)]
-        wtq = [sb(f"wtq{c}", [P, N // 2], U32) for c in range(2)]
-        wts = [sb(f"wts{c}", [P, N // 2], U8) for c in range(2)]
+        wt_raw = sb("wt_raw", [P, 4, N], F32)
+        wt_bf = sb("wt_bf", [P, N, 4], BF16)
+        wts = sb("wts", [P, N], U8)
         r_win = [sb(f"r_win{t}", [P, T], F32) for t in range(NT)]
         b_rows = sb("b_rows", [P, P], F32)
         ident = sb("ident", [P, P], F32)
@@ -62,7 +61,7 @@ def tile_list_gmu_silu_resL_kernel(
         gs1 = sb("gs1", [P, J // 4], I32)
         gs2 = sb("gs2", [P, J], U8)
         gw = sb("gw", [P, J], U32)
-        gsp = sb("gsp", [P, 2, J], U16)
+        gsp = [sb(f"gsp{h}", [P, 2, H], U16) for h in range(2)]
         gw2 = sb("gw2", [P, J], U32)
 
         def row_tiles(name):
@@ -81,29 +80,28 @@ def tile_list_gmu_silu_resL_kernel(
         make_identity(nc, ident[:])
 
         def load_scales(first, count, src):
-            for q in range(4):
-                rows = src[:, 4 * q : 4 * q + 4, :].rearrange("a r n -> r a n").bitcast(I32)
-                nc.sync.dma_start(out=wsc[32 * q : 32 * q + 4, first : first + count, :], in_=rows)
+            rows = src.rearrange("a (q r) n -> r q a n", r=4)
+            for r in range(4):
+                nc.sync.dma_start(out=wsc[r:P:32, first : first + count, :], in_=rows[r].bitcast(I32))
 
         def load_r(t):
             nc.sync.dma_start(out=r_win[t][:], in_=rT[t * P : (t + 1) * P, :])
 
-        wt_v = wt.rearrange("(p j) n -> p j n", j=4)
+        tab2_rows = tab2_scales[0].rearrange("(q r) t -> r q t", r=4)
         tab_rows = tab_scales.rearrange("a (q r) t -> r q a t", r=4)
         nc.sync.dma_start(idx[:], offs)
         nc.sync.dma_start(idx2[:], offs2)
         for r in range(4):
             nc.sync.dma_start(out=tabs[r:P:16, :], in_=tab_rows[r].bitcast(I32))
         nc.sync.dma_start(out=tabw[:], in_=tab_words[0].rearrange("p t b -> p (t b)").bitcast(I32))
+        nc.sync.dma_start(out=wt_raw[:], in_=wt.rearrange("(p j) n -> p j n", j=4))
+        for r in range(4):
+            nc.sync.dma_start(out=tab2s[r:P:32, :], in_=tab2_rows[r].bitcast(I32))
         nc.sync.dma_start(out=tab2w[:], in_=tab2_words[0].rearrange("p t b -> p (t b)").bitcast(I32))
-        for q in range(4):
-            nc.sync.dma_start(out=tab2s[32 * q : 32 * q + 4, :], in_=tab2_scales[0, 4 * q : 4 * q + 4, :].bitcast(I32))
         nc.vector.tensor_copy(gs[:], tabs[:].bitcast(U8).indirect(idx[:]))
         nc.sync.dma_start(out=gs1[0:112, :], in_=gs[16:128, :].bitcast(I32))
         nc.sync.dma_start(out=wvw[:], in_=wv_words.rearrange("a p n -> p a n").bitcast(I32))
-        nc.sync.dma_start(out=wt_raw[0][:], in_=wt_v[:, :, 0 : N // 2])
         load_scales(0, 2, wv_scales)
-        nc.sync.dma_start(out=wt_raw[1][:], in_=wt_v[:, :, N // 2 : N])
         load_r(0)
         load_scales(2, 2, zv_scales)
         nc.sync.dma_start(out=zvw[:], in_=zv_words.rearrange("a p n -> p a n").bitcast(I32))
@@ -122,6 +120,9 @@ def tile_list_gmu_silu_resL_kernel(
         def half(h):
             return slice(h * H, (h + 1) * H)
 
+        def cols(h):
+            return slice(h * (H // 16), (h + 1) * (H // 16))
+
         def tab_plane(h, a):
             return gs[:, half(h)] if a == 0 else gs1[:].bitcast(U8)[:, half(h)]
 
@@ -133,7 +134,7 @@ def tile_list_gmu_silu_resL_kernel(
                 nc.tensor.matmul_mx(
                     out=acc[:], lhsT=words[:, a, t * 64 : (t + 1) * 64].bitcast(FP4X4),
                     lhsT_scale=wplane(first_plane + a, t),
-                    rhs=gsp[:, a, half(h)].bitcast(FP4X4), rhs_scale=tab_plane(h, a), start=(a == 0), stop=(stop and a == 1),
+                    rhs=gsp[h][:, a, :].bitcast(FP4X4), rhs_scale=tab_plane(h, a), start=(a == 0), stop=(stop and a == 1),
                 )
 
         def product_v(h, t):
@@ -143,9 +144,9 @@ def tile_list_gmu_silu_resL_kernel(
 
         def product_t(h, t):
             acc = bank()
-            c = slice((t % 2) * P, (t % 2 + 1) * P)
+            c = slice(t * P, (t + 1) * P)
             nc.tensor.matmul_mx(
-                out=acc[:], lhsT=wtq[t // 2][:, c].bitcast(FP8X4), lhsT_scale=wts[t // 2][:, c],
+                out=acc[:], lhsT=wtq[:, c].bitcast(FP8X4), lhsT_scale=wts[:, c],
                 rhs=gw2[:, half(h)].bitcast(FP8X4), rhs_scale=gs2[:, half(h)], start=True, stop=True,
             )
             nc.scalar.activation(at[t][:, half(h)], acc[:], ACT.Silu)
@@ -159,26 +160,23 @@ def tile_list_gmu_silu_resL_kernel(
             )
             nc.scalar.activation(th[t][:, half(h)], acc[:], ACT.Tanh, bias=b_half[:, t : t + 1], scale=0.5)
 
-        def cast_wt(c):
-            nc.scalar.copy(wt_bf[c][:], wt_raw[c][:].rearrange("p j n -> p n j"))
-
-        def quantise_wt(c):
-            nc.vector.quantize_mx(out=wtq[c][:].bitcast(FP8X4), scales=wts[c][:], in_=wt_bf[c][:].rearrange("p n j -> p (n j)"))
-
-        nc.vector.tensor_copy(gw[:], tabw[:].bitcast(U32).indirect(idx[:]))
-        nc.vector.tensor_copy(gsp[:], gw[:].bitcast(U16).rearrange("p (t d) -> p d t", d=2))
-        nc.vector.tensor_copy(gw2[:], tab2w[:].bitcast(U32).indirect(idx2[:]))
+        for h in range(2):
+            nc.vector.tensor_copy(gw[:, half(h)], tabw[:].bitcast(U32).indirect(idx[:, cols(h)]))
+        for h in range(2):
+            nc.vector.tensor_copy(gsp[h][:], gw[:, half(h)].bitcast(U16).rearrange("p (t d) -> p d t", d=2))
         nc.vector.tensor_copy(gs2[:], tab2s[:].bitcast(U8).indirect(idx2[:]))
-        for c in range(2):
-            cast_wt(c)
-            quantise_wt(c)
+        nc.vector.tensor_copy(gw2[:], tab2w[:].bitcast(U32).indirect(idx2[:]))
+        nc.scalar.copy(wt_bf[:], wt_raw[:].rearrange("p j n -> p n j"))
+        wtq = keep.tile([P, N], U32, name="wtq", tag="tab2s_wtq", align_bytes=64)
+        nc.vector.quantize_mx(out=wtq[:].bitcast(FP8X4), scales=wts[:], in_=wt_bf[:].rearrange("p n j -> p (n j)"))
 
         def both(step, t):
             for h in range(2):
                 step(h, t)
 
         def mix(t):
-            nc.vector.tensor_tensor(uu[t][:], r_win[t][:].indirect(idx[:]), av[t][:], ALU.add)
+            for h in range(2):
+                nc.vector.tensor_tensor(uu[t][:, half(h)], r_win[t][:].indirect(idx[:, cols(h)]), av[t][:, half(h)], ALU.add)
             for h in range(2):
                 nc.vector.tensor_tensor(av[t][:, half(h)], av[t][:, half(h)], at[t][:, half(h)], ALU.subtract)
             for h in range(2):
@@ -206,27 +204,32 @@ def tile_list_gmu_silu_resL_kernel(
             nc.scalar.copy(res[t][:, half(h)], acc[:])
             nc.sync.dma_start(out=out[t * P : (t + 1) * P, half(h)], in_=res[t][:, half(h)])
 
-        for t in range(NT - 1):
-            both(product_v, t)
+        both(product_v, 0)
+        both(product_v, 1)
+        both(product_v, 2)
         both(product_t, 0)
         b_turned = bank()
         nc.tensor.transpose(b_turned[:, 0:P], b_rows[:], ident[:])
         nc.scalar.activation(b_half[:], b_turned[:, 0:NT], ACT.Copy, scale=0.5)
         both(product_z, 0)
         mix(0)
-        both(product_v, NT - 1)
+        both(product_v, 3)
         both(product_t, 1)
         both(product_z, 1)
         mix(1)
-        for t in range(2):
-            both(sum_turned, t)
-            both(product_t, t + 2)
-            both(turn_back, t)
-            both(product_z, t + 2)
-            mix(t + 2)
-            if t == 0:
-                finish_on_vector(2, half(1))
+        both(sum_turned, 0)
+        both(product_t, 2)
+        both(turn_back, 0)
+        both(product_z, 2)
+        mix(2)
+        finish_on_vector(2, half(1))
+        both(sum_turned, 1)
+        both(product_t, 3)
+        both(turn_back, 1)
+        product_z(0, 3)
         sum_turned(0, 2)
+        product_z(1, 3)
         turn_back(0, 2)
+        mix(3)
         for c in (half(0), slice(512, 768), slice(768, J)):
             finish_on_vector(NT - 1, c)

@@ -20,7 +20,13 @@ ALU = mybir.AluOpType
 P = 128
 H = 512
 NT = N // P
-JT = H // P
+BLOCKS = H // P
+QUADRANT = 32
+SHIFT = 16
+BANKS = 8
+WT_COLS = N // 2
+FP4_TILE = P // 2
+WV_PLANE, ZV_PLANE, ZT_PLANE, PLANES = 0, 2, 4, 5
 
 
 def tile_list_gmu_silu_resL_kernel(
@@ -33,56 +39,61 @@ def tile_list_gmu_silu_resL_kernel(
         keep = ctx.enter_context(tc.tile_pool(name="keep", bufs=1))
         psum = ctx.enter_context(tc.psum_pool(name="psum", bufs=1))
 
-        def sb(name, shape, dtype):
-            return keep.tile(shape, dtype, name=name, align_bytes=64)
+        def sb(name, shape, dtype, tag=None):
+            return keep.tile(shape, dtype, name=name, tag=tag or name, align_bytes=64)
 
         idx = lists.tile([P, J // 16], U16, name="idx")
         idx2 = lists.tile([P, J // 16], U16, name="idx2")
 
-        tabs = sb("tabs", [P, T // 4], I32)
-        tab2s = keep.tile([P, T // 4], I32, name="tab2s", tag="tab2s_wtq", align_bytes=64)
-        wsc = sb("wsc", [P, 5, N // 4], I32)
-        tabw = sb("tabw", [P, T], I32)
-        tab2w = sb("tab2w", [P, T], I32)
-        wvw = sb("wvw", [P, 2, N // 2], I32)
-        zvw = sb("zvw", [P, 2, N // 2], I32)
-        ztw = sb("ztw", [P, N // 2], I32)
-        wt_raw = sb("wt_raw", [P, 4, N], F32)
-        wt_bf = sb("wt_bf", [P, N, 4], BF16)
-        wts = sb("wts", [P, N], U8)
+        tab_s = sb("tab_s", [P, T // 4], I32)
+        tab2_s = sb("tab2_s", [P, T // 4], I32, tag="tab2_s_then_wt_codes")
+        w_planes = sb("w_planes", [P, PLANES, N // 4], I32)
+        tab_w = sb("tab_w", [P, T], I32)
+        tab2_w = sb("tab2_w", [P, T], I32)
+        wv_w = sb("wv_w", [P, 2, N // 2], I32)
+        zv_w = sb("zv_w", [P, 2, N // 2], I32)
+        zt_w = sb("zt_w", [P, N // 2], I32)
+        wt_raw = [sb(f"wt_raw{c}", [P, 4, WT_COLS], F32) for c in range(2)]
+        wt_bf = [sb(f"wt_bf{c}", [P, WT_COLS, 4], BF16) for c in range(2)]
+        wt_plane = [sb(f"wt_plane{c}", [P, WT_COLS], U8) for c in range(2)]
         r_win = [sb(f"r_win{t}", [P, T], F32) for t in range(NT)]
         b_rows = sb("b_rows", [P, P], F32)
         ident = sb("ident", [P, P], F32)
         b_half = sb("b_half", [P, NT], F32)
-        warm = sb("warm", [P, 8], F32)
-        warm_o = sb("warm_o", [P, 8], F32)
+        warm_in = sb("warm_in", [P, 8], F32)
+        warm_out = sb("warm_out", [P, 8], F32)
 
-        gs = sb("gs", [P, J], U8)
-        gs1 = sb("gs1", [P, J // 4], I32)
-        gs2 = sb("gs2", [P, J], U8)
-        gw = sb("gw", [P, J], U32)
-        gsp = [sb(f"gsp{h}", [P, 2, H], U16) for h in range(2)]
-        gw2 = sb("gw2", [P, J], U32)
+        v_plane0 = sb("v_plane0", [P, J], U8)
+        v_plane1 = sb("v_plane1", [P, J // 4], I32)
+        v2_plane = sb("v2_plane", [P, J], U8)
+        v_pairs = sb("v_pairs", [P, J], U32)
+        v_codes = [sb(f"v_codes{h}", [P, 2, H], U16) for h in range(2)]
+        v2_codes = sb("v2_codes", [P, J], U32)
 
         def row_tiles(name):
             return [sb(f"{name}{t}", [P, J], F32) for t in range(NT)]
 
-        av, at, th, uu, res = [row_tiles(x) for x in ("av", "at", "th", "uu", "res")]
+        av, at, th, base, res = [row_tiles(x) for x in ("av", "at", "th", "base", "res")]
         turned = [sb(f"turned{t}", [P, J], F32) for t in range(NT - 1)]
+        diff = av
+        prod = th
 
-        nc.gpsimd.memset(tabs[:], 0)
-        nc.vector.memset(tab2s[:], 0)
-        nc.vector.memset(wsc[:], 0)
-        nc.vector.memset(gs1[:], 0)
-        nc.vector.memset(warm[:], 0.0)
-        nc.scalar.activation(warm_o[:], warm[:], ACT.Silu)
+        nc.gpsimd.memset(tab_s[:], 0)
+        nc.vector.memset(tab2_s[:], 0)
+        nc.vector.memset(w_planes[:], 0)
+        nc.vector.memset(v_plane1[:], 0)
+        nc.vector.memset(warm_in[:], 0.0)
+        nc.scalar.activation(warm_out[:], warm_in[:], ACT.Silu)
         nc.vector.memset(b_rows[:], 0.0)
         make_identity(nc, ident[:])
 
-        def load_scales(first, count, src):
+        def load_planes(first, passes, src):
             rows = src.rearrange("a (q r) n -> r q a n", r=4)
             for r in range(4):
-                nc.sync.dma_start(out=wsc[r:P:32, first : first + count, :], in_=rows[r].bitcast(I32))
+                nc.sync.dma_start(out=w_planes[r:P:QUADRANT, first : first + passes, :], in_=rows[r].bitcast(I32))
+
+        def load_wt(c):
+            nc.sync.dma_start(out=wt_raw[c][:], in_=wt.rearrange("(p i) n -> p i n", i=4)[:, :, c * WT_COLS : (c + 1) * WT_COLS])
 
         def load_r(t):
             nc.sync.dma_start(out=r_win[t][:], in_=rT[t * P : (t + 1) * P, :])
@@ -92,83 +103,88 @@ def tile_list_gmu_silu_resL_kernel(
         nc.sync.dma_start(idx[:], offs)
         nc.sync.dma_start(idx2[:], offs2)
         for r in range(4):
-            nc.sync.dma_start(out=tabs[r:P:16, :], in_=tab_rows[r].bitcast(I32))
-        nc.sync.dma_start(out=tabw[:], in_=tab_words[0].rearrange("p t b -> p (t b)").bitcast(I32))
-        nc.sync.dma_start(out=wt_raw[:], in_=wt.rearrange("(p j) n -> p j n", j=4))
+            nc.sync.dma_start(out=tab_s[r:P:SHIFT, :], in_=tab_rows[r].bitcast(I32))
+        nc.sync.dma_start(out=tab_w[:], in_=tab_words[0].rearrange("p t b -> p (t b)").bitcast(I32))
+        nc.sync.dma_start(out=tab2_w[:], in_=tab2_words[0].rearrange("p t b -> p (t b)").bitcast(I32))
         for r in range(4):
-            nc.sync.dma_start(out=tab2s[r:P:32, :], in_=tab2_rows[r].bitcast(I32))
-        nc.sync.dma_start(out=tab2w[:], in_=tab2_words[0].rearrange("p t b -> p (t b)").bitcast(I32))
-        nc.vector.tensor_copy(gs[:], tabs[:].bitcast(U8).indirect(idx[:]))
-        nc.sync.dma_start(out=gs1[0:112, :], in_=gs[16:128, :].bitcast(I32))
-        nc.sync.dma_start(out=wvw[:], in_=wv_words.rearrange("a p n -> p a n").bitcast(I32))
-        load_scales(0, 2, wv_scales)
+            nc.sync.dma_start(out=tab2_s[r:P:QUADRANT, :], in_=tab2_rows[r].bitcast(I32))
+        nc.vector.tensor_copy(v_plane0[:], tab_s[:].bitcast(U8).indirect(idx[:]))
+        nc.sync.dma_start(out=v_plane1[0 : P - SHIFT, :], in_=v_plane0[SHIFT:P, :].bitcast(I32))
+        nc.sync.dma_start(out=wv_w[:], in_=wv_words.rearrange("a p n -> p a n").bitcast(I32))
+        load_wt(0)
+        load_planes(WV_PLANE, 2, wv_scales)
         load_r(0)
-        load_scales(2, 2, zv_scales)
-        nc.sync.dma_start(out=zvw[:], in_=zv_words.rearrange("a p n -> p a n").bitcast(I32))
-        nc.sync.dma_start(out=ztw[:], in_=zt_words[0].bitcast(I32))
-        load_scales(4, 1, zt_scales)
+        load_planes(ZV_PLANE, 2, zv_scales)
+        nc.sync.dma_start(out=zv_w[:], in_=zv_words.rearrange("a p n -> p a n").bitcast(I32))
+        nc.sync.dma_start(out=zt_w[:], in_=zt_words[0].bitcast(I32))
+        load_planes(ZT_PLANE, 1, zt_scales)
         nc.sync.dma_start(out=b_rows[0:NT, :], in_=b.rearrange("(t p) -> t p", p=P))
         load_r(1)
+        load_wt(1)
         load_r(2)
         load_r(3)
 
-        wsc8 = wsc[:].rearrange("p a n -> p (a n)").bitcast(U8)
+        w_bytes = w_planes[:].rearrange("p a n -> p (a n)").bitcast(U8)
 
-        def wplane(a, t):
-            return wsc8[:, a * N + t * P : a * N + (t + 1) * P]
+        def w_plane(place, t):
+            return w_bytes[:, place * N + t * P : place * N + (t + 1) * P]
 
         def half(h):
             return slice(h * H, (h + 1) * H)
 
-        def cols(h):
+        def list_half(h):
             return slice(h * (H // 16), (h + 1) * (H // 16))
 
-        def tab_plane(h, a):
-            return gs[:, half(h)] if a == 0 else gs1[:].bitcast(U8)[:, half(h)]
+        def v_plane(h, a):
+            return v_plane0[:, half(h)] if a == 0 else v_plane1[:].bitcast(U8)[:, half(h)]
 
         def bank():
-            return psum.tile([P, H], F32, name="acc", tag="acc", bufs=8)
+            return psum.tile([P, H], F32, name="acc", tag="acc", bufs=BANKS)
 
-        def tab_passes(acc, words, first_plane, h, t, stop):
+        def v_passes(acc, words, first_plane, h, t, stop):
             for a in range(2):
                 nc.tensor.matmul_mx(
-                    out=acc[:], lhsT=words[:, a, t * 64 : (t + 1) * 64].bitcast(FP4X4),
-                    lhsT_scale=wplane(first_plane + a, t),
-                    rhs=gsp[h][:, a, :].bitcast(FP4X4), rhs_scale=tab_plane(h, a), start=(a == 0), stop=(stop and a == 1),
+                    out=acc[:], lhsT=words[:, a, t * FP4_TILE : (t + 1) * FP4_TILE].bitcast(FP4X4),
+                    lhsT_scale=w_plane(first_plane + a, t),
+                    rhs=v_codes[h][:, a, :].bitcast(FP4X4), rhs_scale=v_plane(h, a), start=(a == 0), stop=(stop and a == 1),
                 )
 
         def product_v(h, t):
             acc = bank()
-            tab_passes(acc, wvw, 0, h, t, True)
+            v_passes(acc, wv_w, WV_PLANE, h, t, True)
             nc.scalar.activation(av[t][:, half(h)], acc[:], ACT.Silu)
 
         def product_t(h, t):
             acc = bank()
-            c = slice(t * P, (t + 1) * P)
+            c = slice((t % 2) * P, (t % 2 + 1) * P)
             nc.tensor.matmul_mx(
-                out=acc[:], lhsT=wtq[:, c].bitcast(FP8X4), lhsT_scale=wts[:, c],
-                rhs=gw2[:, half(h)].bitcast(FP8X4), rhs_scale=gs2[:, half(h)], start=True, stop=True,
+                out=acc[:], lhsT=wt_codes[t // 2][:, c].bitcast(FP8X4), lhsT_scale=wt_plane[t // 2][:, c],
+                rhs=v2_codes[:, half(h)].bitcast(FP8X4), rhs_scale=v2_plane[:, half(h)], start=True, stop=True,
             )
             nc.scalar.activation(at[t][:, half(h)], acc[:], ACT.Silu)
 
         def product_z(h, t):
             acc = bank()
-            tab_passes(acc, zvw, 2, h, t, False)
+            v_passes(acc, zv_w, ZV_PLANE, h, t, False)
             nc.tensor.matmul_mx(
-                out=acc[:], lhsT=ztw[:, t * 64 : (t + 1) * 64].bitcast(FP4X4), lhsT_scale=wplane(4, t),
-                rhs=gw2[:, half(h)].bitcast(FP8X4), rhs_scale=gs2[:, half(h)], start=False, stop=True,
+                out=acc[:], lhsT=zt_w[:, t * FP4_TILE : (t + 1) * FP4_TILE].bitcast(FP4X4), lhsT_scale=w_plane(ZT_PLANE, t),
+                rhs=v2_codes[:, half(h)].bitcast(FP8X4), rhs_scale=v2_plane[:, half(h)], start=False, stop=True,
             )
             nc.scalar.activation(th[t][:, half(h)], acc[:], ACT.Tanh, bias=b_half[:, t : t + 1], scale=0.5)
 
         for h in range(2):
-            nc.vector.tensor_copy(gw[:, half(h)], tabw[:].bitcast(U32).indirect(idx[:, cols(h)]))
+            nc.vector.tensor_copy(v_pairs[:, half(h)], tab_w[:].bitcast(U32).indirect(idx[:, list_half(h)]))
         for h in range(2):
-            nc.vector.tensor_copy(gsp[h][:], gw[:, half(h)].bitcast(U16).rearrange("p (t d) -> p d t", d=2))
-        nc.vector.tensor_copy(gs2[:], tab2s[:].bitcast(U8).indirect(idx2[:]))
-        nc.vector.tensor_copy(gw2[:], tab2w[:].bitcast(U32).indirect(idx2[:]))
-        nc.scalar.copy(wt_bf[:], wt_raw[:].rearrange("p j n -> p n j"))
-        wtq = keep.tile([P, N], U32, name="wtq", tag="tab2s_wtq", align_bytes=64)
-        nc.vector.quantize_mx(out=wtq[:].bitcast(FP8X4), scales=wts[:], in_=wt_bf[:].rearrange("p n j -> p (n j)"))
+            nc.vector.tensor_copy(v_codes[h][:], v_pairs[:, half(h)].bitcast(U16).rearrange("p (t a) -> p a t", a=2))
+        nc.vector.tensor_copy(v2_codes[:], tab2_w[:].bitcast(U32).indirect(idx2[:]))
+        nc.vector.tensor_copy(v2_plane[:], tab2_s[:].bitcast(U8).indirect(idx2[:]))
+        wt_codes = [sb("wt_codes0", [P, WT_COLS], U32, tag="tab2_s_then_wt_codes"), sb("wt_codes1", [P, WT_COLS], U32)]
+
+        def quantise_wt(c):
+            nc.scalar.copy(wt_bf[c][:].rearrange("p (m n) i -> p m i n", n=4), wt_raw[c][:].rearrange("p i (m n) -> p m i n", n=4))
+            nc.vector.quantize_mx(out=wt_codes[c][:].bitcast(FP8X4), scales=wt_plane[c][:], in_=wt_bf[c][:].rearrange("p n i -> p (n i)"))
+
+        quantise_wt(0)
 
         def both(step, t):
             for h in range(2):
@@ -176,29 +192,29 @@ def tile_list_gmu_silu_resL_kernel(
 
         def mix(t):
             for h in range(2):
-                nc.vector.tensor_tensor(uu[t][:, half(h)], r_win[t][:].indirect(idx[:, cols(h)]), av[t][:, half(h)], ALU.add)
+                nc.vector.tensor_tensor(base[t][:, half(h)], r_win[t][:].indirect(idx[:, list_half(h)]), av[t][:, half(h)], ALU.add)
             for h in range(2):
-                nc.vector.tensor_tensor(av[t][:, half(h)], av[t][:, half(h)], at[t][:, half(h)], ALU.subtract)
+                nc.vector.tensor_tensor(diff[t][:, half(h)], av[t][:, half(h)], at[t][:, half(h)], ALU.subtract)
             for h in range(2):
-                nc.vector.scalar_tensor_tensor(th[t][:, half(h)], th[t][:, half(h)], -1.0, av[t][:, half(h)], ALU.add, ALU.mult)
+                nc.vector.scalar_tensor_tensor(prod[t][:, half(h)], th[t][:, half(h)], -1.0, diff[t][:, half(h)], ALU.add, ALU.mult)
 
         def finish_on_vector(t, c):
-            nc.vector.scalar_tensor_tensor(res[t][:, c], th[t][:, c], 0.5, uu[t][:, c], ALU.mult, ALU.add)
+            nc.vector.scalar_tensor_tensor(res[t][:, c], prod[t][:, c], 0.5, base[t][:, c], ALU.mult, ALU.add)
             nc.sync.dma_start(out=out[t * P : (t + 1) * P, c], in_=res[t][:, c])
 
         def sum_turned(h, t):
             acc = bank()
-            for s in range(JT):
+            for s in range(BLOCKS):
                 c = slice(s * P, (s + 1) * P)
                 j = slice(h * H + s * P, h * H + (s + 1) * P)
-                nc.tensor.matmul(acc[:, c], uu[t][:, j], ident[:], start=True, stop=False, is_transpose=True)
-                nc.tensor.matmul(acc[:, c], uu[t][:, j], ident[:], start=False, stop=False, is_transpose=True)
-                nc.tensor.matmul(acc[:, c], th[t][:, j], ident[:], start=False, stop=True, is_transpose=True)
+                nc.tensor.matmul(acc[:, c], base[t][:, j], ident[:], start=True, stop=False, is_transpose=True)
+                nc.tensor.matmul(acc[:, c], base[t][:, j], ident[:], start=False, stop=False, is_transpose=True)
+                nc.tensor.matmul(acc[:, c], prod[t][:, j], ident[:], start=False, stop=True, is_transpose=True)
             nc.scalar.activation(turned[t][:, half(h)], acc[:], ACT.Copy, scale=0.5)
 
         def turn_back(h, t):
             acc = bank()
-            for s in range(JT):
+            for s in range(BLOCKS):
                 j = slice(h * H + s * P, h * H + (s + 1) * P)
                 nc.tensor.transpose(acc[:, s * P : (s + 1) * P], turned[t][:, j], ident[:])
             nc.scalar.copy(res[t][:, half(h)], acc[:])
@@ -213,14 +229,16 @@ def tile_list_gmu_silu_resL_kernel(
         nc.scalar.activation(b_half[:], b_turned[:, 0:NT], ACT.Copy, scale=0.5)
         both(product_z, 0)
         mix(0)
+        quantise_wt(1)
         both(product_v, 3)
         both(product_t, 1)
         both(product_z, 1)
         mix(1)
         both(sum_turned, 0)
-        both(product_t, 2)
+        product_z(0, 2)
         both(turn_back, 0)
-        both(product_z, 2)
+        product_z(1, 2)
+        both(product_t, 2)
         mix(2)
         finish_on_vector(2, half(1))
         both(sum_turned, 1)
@@ -231,5 +249,5 @@ def tile_list_gmu_silu_resL_kernel(
         product_z(1, 3)
         turn_back(0, 2)
         mix(3)
-        for c in (half(0), slice(512, 768), slice(768, J)):
+        for c in (half(0), slice(H, H + H // 2), slice(H + H // 2, J)):
             finish_on_vector(NT - 1, c)

@@ -65,8 +65,7 @@ def tile_list_gmu_silu_resL_kernel(
 
         v_plane0 = sb("v_plane0", [P, J], U8)
         v_plane1 = sb("v_plane1", [P, J // 4], I32)
-        v2_plane = sb("v2_plane", [P, J], U8)
-        v_pairs = sb("v_pairs", [P, J], U32)
+        v_pairs = sb("v_pairs", [P, J], U32, tag="pairs_then_v2_plane")
         v_codes = [sb(f"v_codes{h}", [P, 2, H], U16) for h in range(2)]
         v2_codes = sb("v2_codes", [P, J], U32)
 
@@ -85,7 +84,6 @@ def tile_list_gmu_silu_resL_kernel(
         nc.vector.memset(warm_in[:], 0.0)
         nc.scalar.activation(warm_out[:], warm_in[:], ACT.Silu)
         nc.vector.memset(b_rows[:], 0.0)
-        make_identity(nc, ident[:])
 
         def load_planes(first, passes, src):
             rows = src.rearrange("a (q r) n -> r q a n", r=4)
@@ -107,11 +105,11 @@ def tile_list_gmu_silu_resL_kernel(
         nc.sync.dma_start(out=tab_w[:], in_=tab_words[0].rearrange("p t b -> p (t b)").bitcast(I32))
         nc.sync.dma_start(out=tab2_w[:], in_=tab2_words[0].rearrange("p t b -> p (t b)").bitcast(I32))
         for r in range(4):
-            nc.sync.dma_start(out=tab2_s[r:P:QUADRANT, :], in_=tab2_rows[r].bitcast(I32))
-        nc.vector.tensor_copy(v_plane0[:], tab_s[:].bitcast(U8).indirect(idx[:]))
-        nc.sync.dma_start(out=v_plane1[0 : P - SHIFT, :], in_=v_plane0[SHIFT:P, :].bitcast(I32))
+            nc.gpsimd.dma_start(out=tab2_s[r:P:QUADRANT, :], in_=tab2_rows[r].bitcast(I32))
         nc.sync.dma_start(out=wv_w[:], in_=wv_words.rearrange("a p n -> p a n").bitcast(I32))
         load_wt(0)
+        nc.vector.tensor_copy(v_plane0[:], tab_s[:].bitcast(U8).indirect(idx[:]))
+        nc.sync.dma_start(out=v_plane1[0 : P - SHIFT, :], in_=v_plane0[SHIFT:P, :].bitcast(I32))
         load_planes(WV_PLANE, 2, wv_scales)
         load_r(0)
         load_planes(ZV_PLANE, 2, zv_scales)
@@ -123,6 +121,7 @@ def tile_list_gmu_silu_resL_kernel(
         load_wt(1)
         load_r(2)
         load_r(3)
+        make_identity(nc, ident[:])
 
         w_bytes = w_planes[:].rearrange("p a n -> p (a n)").bitcast(U8)
 
@@ -177,6 +176,7 @@ def tile_list_gmu_silu_resL_kernel(
         for h in range(2):
             nc.vector.tensor_copy(v_codes[h][:], v_pairs[:, half(h)].bitcast(U16).rearrange("p (t a) -> p a t", a=2))
         nc.vector.tensor_copy(v2_codes[:], tab2_w[:].bitcast(U32).indirect(idx2[:]))
+        v2_plane = sb("v2_plane", [P, J], U8, tag="pairs_then_v2_plane")
         nc.vector.tensor_copy(v2_plane[:], tab2_s[:].bitcast(U8).indirect(idx2[:]))
         wt_codes = [sb("wt_codes0", [P, WT_COLS], U32, tag="tab2_s_then_wt_codes"), sb("wt_codes1", [P, WT_COLS], U32)]
 

@@ -74,7 +74,7 @@ def tile_list_gmu_silu_resL_kernel(
 
         av, at, th, base, res = [row_tiles(x) for x in ("av", "at", "th", "base", "res")]
         turned = [sb(f"turned{t}", [P, J], F32) for t in range(NT - 1)]
-        diff = av
+        diff = at
         prod = th
 
         nc.gpsimd.memset(tab_s[:], 0)
@@ -190,35 +190,40 @@ def tile_list_gmu_silu_resL_kernel(
             for h in range(2):
                 step(h, t)
 
+        def product(t, c):
+            nc.vector.scalar_tensor_tensor(prod[t][:, c], th[t][:, c], -1.0, diff[t][:, c], ALU.add, ALU.mult)
+
         def mix(t):
-            for h in range(2):
-                nc.vector.tensor_tensor(base[t][:, half(h)], r_win[t][:].indirect(idx[:, list_half(h)]), av[t][:, half(h)], ALU.add)
+            nc.vector.tensor_tensor(base[t][:], r_win[t][:].indirect(idx[:]), av[t][:], ALU.add)
             for h in range(2):
                 nc.vector.tensor_tensor(diff[t][:, half(h)], av[t][:, half(h)], at[t][:, half(h)], ALU.subtract)
-            for h in range(2):
-                nc.vector.scalar_tensor_tensor(prod[t][:, half(h)], th[t][:, half(h)], -1.0, diff[t][:, half(h)], ALU.add, ALU.mult)
+            if t < NT - 1:
+                for h in range(2):
+                    product(t, half(h))
 
         def finish_on_vector(t, c):
             nc.vector.scalar_tensor_tensor(res[t][:, c], prod[t][:, c], 0.5, base[t][:, c], ALU.mult, ALU.add)
             nc.sync.dma_start(out=out[t * P : (t + 1) * P, c], in_=res[t][:, c])
 
-        def sum_turned(h, t):
+        def sum_turned(h, t, blocks=BLOCKS):
             acc = bank()
-            for s in range(BLOCKS):
+            for s in range(blocks):
                 c = slice(s * P, (s + 1) * P)
                 j = slice(h * H + s * P, h * H + (s + 1) * P)
                 nc.tensor.matmul(acc[:, c], base[t][:, j], ident[:], start=True, stop=False, is_transpose=True)
                 nc.tensor.matmul(acc[:, c], base[t][:, j], ident[:], start=False, stop=False, is_transpose=True)
                 nc.tensor.matmul(acc[:, c], prod[t][:, j], ident[:], start=False, stop=True, is_transpose=True)
-            nc.scalar.activation(turned[t][:, half(h)], acc[:], ACT.Copy, scale=0.5)
+            nc.scalar.activation(turned[t][:, h * H : h * H + blocks * P], acc[:, 0 : blocks * P], ACT.Copy, scale=0.5)
 
-        def turn_back(h, t):
+        def turn_back(h, t, blocks=BLOCKS):
+            queue = nc.scalar if t == 2 else nc.sync
             acc = bank()
-            for s in range(BLOCKS):
+            for s in range(blocks):
                 j = slice(h * H + s * P, h * H + (s + 1) * P)
                 nc.tensor.transpose(acc[:, s * P : (s + 1) * P], turned[t][:, j], ident[:])
-            nc.scalar.copy(res[t][:, half(h)], acc[:])
-            nc.sync.dma_start(out=out[t * P : (t + 1) * P, half(h)], in_=res[t][:, half(h)])
+            c = slice(h * H, h * H + blocks * P)
+            nc.scalar.copy(res[t][:, c], acc[:, 0 : blocks * P])
+            queue.dma_start(out=out[t * P : (t + 1) * P, c], in_=res[t][:, c])
 
         both(product_v, 0)
         both(product_v, 1)
@@ -240,14 +245,18 @@ def tile_list_gmu_silu_resL_kernel(
         product_z(1, 2)
         both(product_t, 2)
         mix(2)
-        finish_on_vector(2, half(1))
+        finish_on_vector(2, slice(H // 2, J))
         both(sum_turned, 1)
         both(product_t, 3)
         both(turn_back, 1)
         product_z(0, 3)
-        sum_turned(0, 2)
         product_z(1, 3)
-        turn_back(0, 2)
+        sum_turned(0, 2, BLOCKS // 2)
+        turn_back(0, 2, BLOCKS // 2)
         mix(3)
-        for c in (half(0), slice(H, H + H // 2), slice(H + H // 2, J)):
+        pieces = (half(0), slice(H, H + H // 2), slice(H + H // 2, J))
+        product(NT - 1, pieces[0])
+        for n, c in enumerate(pieces):
+            if n + 1 < len(pieces):
+                product(NT - 1, pieces[n + 1])
             finish_on_vector(NT - 1, c)

@@ -73,7 +73,7 @@ def tile_list_gmu_silu_resL_kernel(
             return [sb(f"{name}{t}", [P, J], F32) for t in range(NT)]
 
         av, at, th, base, res = [row_tiles(x) for x in ("av", "at", "th", "base", "res")]
-        turned = [sb(f"turned{t}", [P, J], F32) for t in range(NT - 1)]
+        turned = [sb(f"turned{t}", [P, J], F32) for t in range(2)]
         diff = at
         prod = th
 
@@ -205,25 +205,23 @@ def tile_list_gmu_silu_resL_kernel(
             nc.vector.scalar_tensor_tensor(res[t][:, c], prod[t][:, c], 0.5, base[t][:, c], ALU.mult, ALU.add)
             nc.sync.dma_start(out=out[t * P : (t + 1) * P, c], in_=res[t][:, c])
 
-        def sum_turned(h, t, blocks=BLOCKS):
+        def sum_turned(h, t):
             acc = bank()
-            for s in range(blocks):
+            for s in range(BLOCKS):
                 c = slice(s * P, (s + 1) * P)
                 j = slice(h * H + s * P, h * H + (s + 1) * P)
                 nc.tensor.matmul(acc[:, c], base[t][:, j], ident[:], start=True, stop=False, is_transpose=True)
                 nc.tensor.matmul(acc[:, c], base[t][:, j], ident[:], start=False, stop=False, is_transpose=True)
                 nc.tensor.matmul(acc[:, c], prod[t][:, j], ident[:], start=False, stop=True, is_transpose=True)
-            nc.scalar.activation(turned[t][:, h * H : h * H + blocks * P], acc[:, 0 : blocks * P], ACT.Copy, scale=0.5)
+            nc.scalar.activation(turned[t][:, half(h)], acc[:], ACT.Copy, scale=0.5)
 
-        def turn_back(h, t, blocks=BLOCKS):
-            queue = nc.scalar if t == 2 else nc.sync
+        def turn_back(h, t):
             acc = bank()
-            for s in range(blocks):
+            for s in range(BLOCKS):
                 j = slice(h * H + s * P, h * H + (s + 1) * P)
                 nc.tensor.transpose(acc[:, s * P : (s + 1) * P], turned[t][:, j], ident[:])
-            c = slice(h * H, h * H + blocks * P)
-            nc.scalar.copy(res[t][:, c], acc[:, 0 : blocks * P])
-            queue.dma_start(out=out[t * P : (t + 1) * P, c], in_=res[t][:, c])
+            nc.scalar.copy(res[t][:, half(h)], acc[:])
+            nc.sync.dma_start(out=out[t * P : (t + 1) * P, half(h)], in_=res[t][:, half(h)])
 
         both(product_v, 0)
         both(product_v, 1)
@@ -245,14 +243,13 @@ def tile_list_gmu_silu_resL_kernel(
         product_z(1, 2)
         both(product_t, 2)
         mix(2)
-        finish_on_vector(2, slice(H // 2, J))
+        for h in range(2):
+            finish_on_vector(2, half(h))
         both(sum_turned, 1)
         both(product_t, 3)
         both(turn_back, 1)
         product_z(0, 3)
         product_z(1, 3)
-        sum_turned(0, 2, BLOCKS // 2)
-        turn_back(0, 2, BLOCKS // 2)
         mix(3)
         pieces = (half(0), slice(H, H + H // 2), slice(H + H // 2, J))
         product(NT - 1, pieces[0])

@@ -22,7 +22,7 @@ H = 512
 NT = N // P
 BLOCKS = H // P
 QUADRANT = 32
-SHIFT = 16
+ROWS = 16
 BANKS = 8
 WT_COLS = N // 2
 FP4_TILE = P // 2
@@ -60,14 +60,13 @@ def tile_list_gmu_silu_resL_kernel(
         b_rows = sb("b_rows", [P, P], F32)
         ident = sb("ident", [P, P], F32)
         b_half = sb("b_half", [P, NT], F32)
-        warm_in = sb("warm_in", [P, 8], F32)
-        warm_out = sb("warm_out", [P, 8], F32)
 
-        v_plane0 = sb("v_plane0", [P, J], U8)
-        v_plane1 = sb("v_plane1", [P, J // 4], I32)
-        v_pairs = sb("v_pairs", [P, J], U32, tag="pairs_then_v2_plane")
+        v_rows = sb("v_rows", [P, J], U8)
+        v_planes = sb("v_planes", [P, 2, J // 4], I32)
+        v_pairs = sb("v_pairs", [P, J], U32)
         v_codes = [sb(f"v_codes{h}", [P, 2, H], U16) for h in range(2)]
         v2_codes = sb("v2_codes", [P, J], U32)
+        v2_plane = sb("v2_plane", [P, J], U8)
 
         def row_tiles(name):
             return [sb(f"{name}{t}", [P, J], F32) for t in range(NT)]
@@ -77,18 +76,16 @@ def tile_list_gmu_silu_resL_kernel(
         diff = at
         prod = th
 
-        nc.gpsimd.memset(tab_s[:], 0)
+        nc.gpsimd.memset(w_planes[:], 0)
+        make_identity(nc, ident[:])
+        nc.gpsimd.memset(v_planes[:], 0)
+        nc.vector.memset(tab_s[QUADRANT : 2 * QUADRANT, :], 0)
+        nc.vector.memset(tab_s[2 * QUADRANT : P, :], 0)
         nc.vector.memset(tab2_s[:], 0)
-        nc.vector.memset(w_planes[:], 0)
-        nc.vector.memset(v_plane1[:], 0)
-        nc.vector.memset(warm_in[:], 0.0)
-        nc.scalar.activation(warm_out[:], warm_in[:], ACT.Silu)
         nc.vector.memset(b_rows[:], 0.0)
 
-        def load_planes(first, passes, src):
-            rows = src.rearrange("a (q r) n -> r q a n", r=4)
-            for r in range(4):
-                nc.sync.dma_start(out=w_planes[r:P:QUADRANT, first : first + passes, :], in_=rows[r].bitcast(I32))
+        def load_rows(first, passes, src):
+            nc.sync.dma_start(out=w_planes[0:ROWS, first : first + passes, :], in_=src.rearrange("a g n -> g a n").bitcast(I32))
 
         def load_wt(c):
             nc.sync.dma_start(out=wt_raw[c][:], in_=wt.rearrange("(p i) n -> p i n", i=4)[:, :, c * WT_COLS : (c + 1) * WT_COLS])
@@ -96,34 +93,35 @@ def tile_list_gmu_silu_resL_kernel(
         def load_r(t):
             nc.sync.dma_start(out=r_win[t][:], in_=rT[t * P : (t + 1) * P, :])
 
-        tab2_rows = tab2_scales[0].rearrange("(q r) t -> r q t", r=4)
-        tab_rows = tab_scales.rearrange("a (q r) t -> r q a t", r=4)
         nc.sync.dma_start(idx[:], offs)
-        nc.sync.dma_start(idx2[:], offs2)
-        for r in range(4):
-            nc.sync.dma_start(out=tab_s[r:P:SHIFT, :], in_=tab_rows[r].bitcast(I32))
+        nc.sync.dma_start(out=tab_s[0 : 2 * ROWS, :], in_=tab_scales.rearrange("a g t -> g a t").bitcast(I32))
         nc.sync.dma_start(out=tab_w[:], in_=tab_words[0].rearrange("p t b -> p (t b)").bitcast(I32))
-        nc.sync.dma_start(out=tab2_w[:], in_=tab2_words[0].rearrange("p t b -> p (t b)").bitcast(I32))
-        for r in range(4):
-            nc.gpsimd.dma_start(out=tab2_s[r:P:QUADRANT, :], in_=tab2_rows[r].bitcast(I32))
+        nc.sync.dma_start(idx2[:], offs2)
+        load_rows(WV_PLANE, 2, wv_scales)
+        load_rows(ZV_PLANE, 2, zv_scales)
+        load_rows(ZT_PLANE, 1, zt_scales)
         nc.sync.dma_start(out=wv_w[:], in_=wv_words.rearrange("a p n -> p a n").bitcast(I32))
+        nc.sync.dma_start(out=tab2_w[:], in_=tab2_words[0].rearrange("p t b -> p (t b)").bitcast(I32))
+        for q in range(1, 4):
+            nc.sync.dma_start(out=w_planes[q * QUADRANT : q * QUADRANT + 4, :, :], in_=w_planes[4 * q : 4 * q + 4, :, :])
+        nc.vector.tensor_copy(v_rows[:], tab_s[:].bitcast(U8).indirect(idx[:]))
+        for q in range(4):
+            nc.sync.dma_start(out=v_planes[q * QUADRANT : q * QUADRANT + 4, :, :], in_=v_rows[8 * q : 8 * q + 8, :].bitcast(I32))
         load_wt(0)
-        nc.vector.tensor_copy(v_plane0[:], tab_s[:].bitcast(U8).indirect(idx[:]))
-        nc.sync.dma_start(out=v_plane1[0 : P - SHIFT, :], in_=v_plane0[SHIFT:P, :].bitcast(I32))
-        load_planes(WV_PLANE, 2, wv_scales)
+        tab2_rows = tab2_scales[0].rearrange("(q r) t -> r q t", r=4)
+        for r in range(4):
+            nc.sync.dma_start(out=tab2_s[r:P:QUADRANT, :], in_=tab2_rows[r].bitcast(I32))
         load_r(0)
-        load_planes(ZV_PLANE, 2, zv_scales)
         nc.sync.dma_start(out=zv_w[:], in_=zv_words.rearrange("a p n -> p a n").bitcast(I32))
         nc.sync.dma_start(out=zt_w[:], in_=zt_words[0].bitcast(I32))
-        load_planes(ZT_PLANE, 1, zt_scales)
         nc.sync.dma_start(out=b_rows[0:NT, :], in_=b.rearrange("(t p) -> t p", p=P))
         load_r(1)
         load_wt(1)
         load_r(2)
         load_r(3)
-        make_identity(nc, ident[:])
 
         w_bytes = w_planes[:].rearrange("p a n -> p (a n)").bitcast(U8)
+        v_bytes = v_planes[:].rearrange("p a n -> p (a n)").bitcast(U8)
 
         def w_plane(place, t):
             return w_bytes[:, place * N + t * P : place * N + (t + 1) * P]
@@ -134,9 +132,6 @@ def tile_list_gmu_silu_resL_kernel(
         def list_half(h):
             return slice(h * (H // 16), (h + 1) * (H // 16))
 
-        def v_plane(h, a):
-            return v_plane0[:, half(h)] if a == 0 else v_plane1[:].bitcast(U8)[:, half(h)]
-
         def bank():
             return psum.tile([P, H], F32, name="acc", tag="acc", bufs=BANKS)
 
@@ -145,7 +140,8 @@ def tile_list_gmu_silu_resL_kernel(
                 nc.tensor.matmul_mx(
                     out=acc[:], lhsT=words[:, a, t * FP4_TILE : (t + 1) * FP4_TILE].bitcast(FP4X4),
                     lhsT_scale=w_plane(first_plane + a, t),
-                    rhs=v_codes[h][:, a, :].bitcast(FP4X4), rhs_scale=v_plane(h, a), start=(a == 0), stop=(stop and a == 1),
+                    rhs=v_codes[h][:, a, :].bitcast(FP4X4), rhs_scale=v_bytes[:, a * J + h * H : a * J + (h + 1) * H],
+                    start=(a == 0), stop=(stop and a == 1),
                 )
 
         def product_v(h, t):
@@ -176,15 +172,13 @@ def tile_list_gmu_silu_resL_kernel(
         for h in range(2):
             nc.vector.tensor_copy(v_codes[h][:], v_pairs[:, half(h)].bitcast(U16).rearrange("p (t a) -> p a t", a=2))
         nc.vector.tensor_copy(v2_codes[:], tab2_w[:].bitcast(U32).indirect(idx2[:]))
-        v2_plane = sb("v2_plane", [P, J], U8, tag="pairs_then_v2_plane")
         nc.vector.tensor_copy(v2_plane[:], tab2_s[:].bitcast(U8).indirect(idx2[:]))
+
         wt_codes = [sb("wt_codes0", [P, WT_COLS], U32, tag="tab2_s_then_wt_codes"), sb("wt_codes1", [P, WT_COLS], U32)]
 
         def quantise_wt(c):
             nc.scalar.copy(wt_bf[c][:].rearrange("p (m n) i -> p m i n", n=4), wt_raw[c][:].rearrange("p i (m n) -> p m i n", n=4))
             nc.vector.quantize_mx(out=wt_codes[c][:].bitcast(FP8X4), scales=wt_plane[c][:], in_=wt_bf[c][:].rearrange("p n i -> p (n i)"))
-
-        quantise_wt(0)
 
         def both(step, t):
             for h in range(2):
@@ -223,9 +217,17 @@ def tile_list_gmu_silu_resL_kernel(
             nc.scalar.copy(res[t][:, half(h)], acc[:])
             nc.sync.dma_start(out=out[t * P : (t + 1) * P, half(h)], in_=res[t][:, half(h)])
 
-        both(product_v, 0)
-        both(product_v, 1)
-        both(product_v, 2)
+        def last_tile():
+            pieces = (half(0), slice(H, H + H // 2), slice(H + H // 2, J))
+            product(NT - 1, pieces[0])
+            for n, c in enumerate(pieces):
+                if n + 1 < len(pieces):
+                    product(NT - 1, pieces[n + 1])
+                finish_on_vector(NT - 1, c)
+
+        quantise_wt(0)
+        for t in range(NT):
+            both(product_v, t)
         both(product_t, 0)
         b_turned = bank()
         nc.tensor.transpose(b_turned[:, 0:P], b_rows[:], ident[:])
@@ -233,7 +235,6 @@ def tile_list_gmu_silu_resL_kernel(
         both(product_z, 0)
         mix(0)
         quantise_wt(1)
-        both(product_v, 3)
         both(product_t, 1)
         both(product_z, 1)
         mix(1)
@@ -251,9 +252,4 @@ def tile_list_gmu_silu_resL_kernel(
         product_z(0, 3)
         product_z(1, 3)
         mix(3)
-        pieces = (half(0), slice(H, H + H // 2), slice(H + H // 2, J))
-        product(NT - 1, pieces[0])
-        for n, c in enumerate(pieces):
-            if n + 1 < len(pieces):
-                product(NT - 1, pieces[n + 1])
-            finish_on_vector(NT - 1, c)
+        last_tile()

@@ -45,7 +45,7 @@ def tile_list_gmu_silu_resL_kernel(
         idx = lists.tile([P, J // 16], U16, name="idx")
         idx2 = lists.tile([P, J // 16], U16, name="idx2")
 
-        tab_s = sb("tab_s", [P, T // 4], I32)
+        tab_s = sb("tab_s", [P, T // 4], I32, tag="tab_s_then_planes")
         tab2_s = sb("tab2_s", [P, T // 4], I32, tag="tab2_s_then_wt_codes")
         w_planes = sb("w_planes", [P, PLANES, N // 4], I32)
         tab_w = sb("tab_w", [P, T], I32)
@@ -61,8 +61,10 @@ def tile_list_gmu_silu_resL_kernel(
         ident = sb("ident", [P, P], F32)
         b_half = sb("b_half", [P, NT], F32)
 
+        warm_in = sb("warm_in", [P, 8], F32)
+        warm_out = sb("warm_out", [P, 8], F32)
+
         v_rows = sb("v_rows", [P, J], U8)
-        v_planes = sb("v_planes", [P, 2, J // 4], I32)
         v_pairs = sb("v_pairs", [P, J], U32)
         v_codes = [sb(f"v_codes{h}", [P, 2, H], U16) for h in range(2)]
         v2_codes = sb("v2_codes", [P, J], U32)
@@ -76,12 +78,13 @@ def tile_list_gmu_silu_resL_kernel(
         diff = at
         prod = th
 
-        nc.gpsimd.memset(w_planes[:], 0)
         make_identity(nc, ident[:])
-        nc.gpsimd.memset(v_planes[:], 0)
+        nc.gpsimd.memset(tab2_s[:], 0)
+        nc.vector.memset(w_planes[:], 0)
         nc.vector.memset(tab_s[QUADRANT : 2 * QUADRANT, :], 0)
         nc.vector.memset(tab_s[2 * QUADRANT : P, :], 0)
-        nc.vector.memset(tab2_s[:], 0)
+        nc.vector.memset(warm_in[:], 0.0)
+        nc.scalar.activation(warm_out[:], warm_in[:], ACT.Silu)
         nc.vector.memset(b_rows[:], 0.0)
 
         def load_rows(first, passes, src):
@@ -97,6 +100,9 @@ def tile_list_gmu_silu_resL_kernel(
         nc.sync.dma_start(out=tab_s[0 : 2 * ROWS, :], in_=tab_scales.rearrange("a g t -> g a t").bitcast(I32))
         nc.sync.dma_start(out=tab_w[:], in_=tab_words[0].rearrange("p t b -> p (t b)").bitcast(I32))
         nc.sync.dma_start(idx2[:], offs2)
+        tab2_rows = tab2_scales[0].rearrange("(q r) t -> r q t", r=4)
+        for r in range(2):
+            nc.gpsimd.dma_start(out=tab2_s[r:P:QUADRANT, :], in_=tab2_rows[r].bitcast(I32))
         load_rows(WV_PLANE, 2, wv_scales)
         load_rows(ZV_PLANE, 2, zv_scales)
         load_rows(ZT_PLANE, 1, zt_scales)
@@ -105,11 +111,11 @@ def tile_list_gmu_silu_resL_kernel(
         for q in range(1, 4):
             nc.sync.dma_start(out=w_planes[q * QUADRANT : q * QUADRANT + 4, :, :], in_=w_planes[4 * q : 4 * q + 4, :, :])
         nc.vector.tensor_copy(v_rows[:], tab_s[:].bitcast(U8).indirect(idx[:]))
+        v_planes = sb("v_planes", [P, 2, J // 4], I32, tag="tab_s_then_planes")
         for q in range(4):
             nc.sync.dma_start(out=v_planes[q * QUADRANT : q * QUADRANT + 4, :, :], in_=v_rows[8 * q : 8 * q + 8, :].bitcast(I32))
         load_wt(0)
-        tab2_rows = tab2_scales[0].rearrange("(q r) t -> r q t", r=4)
-        for r in range(4):
+        for r in range(2, 4):
             nc.sync.dma_start(out=tab2_s[r:P:QUADRANT, :], in_=tab2_rows[r].bitcast(I32))
         load_r(0)
         nc.sync.dma_start(out=zv_w[:], in_=zv_words.rearrange("a p n -> p a n").bitcast(I32))
@@ -226,7 +232,7 @@ def tile_list_gmu_silu_resL_kernel(
                 finish_on_vector(NT - 1, c)
 
         quantise_wt(0)
-        for t in range(NT):
+        for t in range(NT - 1):
             both(product_v, t)
         both(product_t, 0)
         b_turned = bank()
@@ -235,6 +241,7 @@ def tile_list_gmu_silu_resL_kernel(
         both(product_z, 0)
         mix(0)
         quantise_wt(1)
+        both(product_v, 3)
         both(product_t, 1)
         both(product_z, 1)
         mix(1)

@@ -46,14 +46,14 @@ def tile_list_gmu_silu_resL_kernel(
         idx2 = lists.tile([P, J // 16], U16, name="idx2")
 
         tab_s = sb("tab_s", [P, T // 4], I32, tag="tab_s_then_planes")
-        tab2_s = sb("tab2_s", [P, T // 4], I32, tag="tab2_s_then_wt_codes")
+        tab2_s = sb("tab2_s", [P, T // 4], I32)
         w_planes = sb("w_planes", [P, PLANES, N // 4], I32)
         tab_w = sb("tab_w", [P, T], I32)
         tab2_w = sb("tab2_w", [P, T], I32)
         wv_w = sb("wv_w", [P, 2, N // 2], I32)
         zv_w = sb("zv_w", [P, 2, N // 2], I32)
         zt_w = sb("zt_w", [P, N // 2], I32)
-        wt_raw = [sb(f"wt_raw{c}", [P, 4, WT_COLS], F32) for c in range(2)]
+        wt_raw = [sb("wt_raw0", [P, 4, WT_COLS], F32, tag="wt_raw_then_av"), sb("wt_raw1", [P, 4, WT_COLS], F32)]
         wt_bf = [sb(f"wt_bf{c}", [P, WT_COLS, 4], BF16) for c in range(2)]
         wt_plane = [sb(f"wt_plane{c}", [P, WT_COLS], U8) for c in range(2)]
         r_win = [sb(f"r_win{t}", [P, T], F32) for t in range(NT)]
@@ -73,16 +73,21 @@ def tile_list_gmu_silu_resL_kernel(
         def row_tiles(name):
             return [sb(f"{name}{t}", [P, J], F32) for t in range(NT)]
 
-        av, at, th, base, res = [row_tiles(x) for x in ("av", "at", "th", "base", "res")]
+        at, th, base, res = [row_tiles(x) for x in ("at", "th", "base", "res")]
+        av = {t: sb(f"av{t}", [P, J], F32) for t in (0, 2, 3)}
         turned = [sb(f"turned{t}", [P, J], F32) for t in range(2)]
         diff = at
         prod = th
 
-        make_identity(nc, ident[:])
+        def zero_on_vector(rows):
+            cut = rows.shape[1] // 2 + 1
+            nc.vector.memset(rows[:, 0:cut], 0)
+            nc.vector.memset(rows[:, cut:], 0)
+
         nc.gpsimd.memset(tab2_s[:], 0)
-        nc.vector.memset(w_planes[:], 0)
-        nc.vector.memset(tab_s[QUADRANT : 2 * QUADRANT, :], 0)
-        nc.vector.memset(tab_s[2 * QUADRANT : P, :], 0)
+        zero_on_vector(w_planes[:].rearrange("p a n -> p (a n)"))
+        zero_on_vector(tab_s[QUADRANT : 2 * QUADRANT, :])
+        zero_on_vector(tab_s[2 * QUADRANT : P, :])
         nc.vector.memset(warm_in[:], 0.0)
         nc.scalar.activation(warm_out[:], warm_in[:], ACT.Silu)
         nc.vector.memset(b_rows[:], 0.0)
@@ -114,9 +119,9 @@ def tile_list_gmu_silu_resL_kernel(
         v_planes = sb("v_planes", [P, 2, J // 4], I32, tag="tab_s_then_planes")
         for q in range(4):
             nc.sync.dma_start(out=v_planes[q * QUADRANT : q * QUADRANT + 4, :, :], in_=v_rows[8 * q : 8 * q + 8, :].bitcast(I32))
-        load_wt(0)
         for r in range(2, 4):
             nc.sync.dma_start(out=tab2_s[r:P:QUADRANT, :], in_=tab2_rows[r].bitcast(I32))
+        load_wt(0)
         load_r(0)
         nc.sync.dma_start(out=zv_w[:], in_=zv_words.rearrange("a p n -> p a n").bitcast(I32))
         nc.sync.dma_start(out=zt_w[:], in_=zt_words[0].bitcast(I32))
@@ -125,6 +130,8 @@ def tile_list_gmu_silu_resL_kernel(
         load_wt(1)
         load_r(2)
         load_r(3)
+
+        make_identity(nc, ident[:])
 
         w_bytes = w_planes[:].rearrange("p a n -> p (a n)").bitcast(U8)
         v_bytes = v_planes[:].rearrange("p a n -> p (a n)").bitcast(U8)
@@ -180,7 +187,7 @@ def tile_list_gmu_silu_resL_kernel(
         nc.vector.tensor_copy(v2_codes[:], tab2_w[:].bitcast(U32).indirect(idx2[:]))
         nc.vector.tensor_copy(v2_plane[:], tab2_s[:].bitcast(U8).indirect(idx2[:]))
 
-        wt_codes = [sb("wt_codes0", [P, WT_COLS], U32, tag="tab2_s_then_wt_codes"), sb("wt_codes1", [P, WT_COLS], U32)]
+        wt_codes = [sb(f"wt_codes{c}", [P, WT_COLS], U32) for c in range(2)]
 
         def quantise_wt(c):
             nc.scalar.copy(wt_bf[c][:].rearrange("p (m n) i -> p m i n", n=4), wt_raw[c][:].rearrange("p i (m n) -> p m i n", n=4))
@@ -232,6 +239,7 @@ def tile_list_gmu_silu_resL_kernel(
                 finish_on_vector(NT - 1, c)
 
         quantise_wt(0)
+        av[1] = sb("av1", [P, J], F32, tag="wt_raw_then_av")
         for t in range(NT - 1):
             both(product_v, t)
         both(product_t, 0)

@@ -111,8 +111,8 @@ def tile_list_gmu_silu_resL_kernel(
         load_rows(WV_PLANE, 2, wv_scales)
         load_rows(ZV_PLANE, 2, zv_scales)
         load_rows(ZT_PLANE, 1, zt_scales)
-        nc.sync.dma_start(out=wv_w[:], in_=wv_words.rearrange("a p n -> p a n").bitcast(I32))
         nc.sync.dma_start(out=tab2_w[:], in_=tab2_words[0].rearrange("p t b -> p (t b)").bitcast(I32))
+        nc.sync.dma_start(out=wv_w[:], in_=wv_words.rearrange("a p n -> p a n").bitcast(I32))
         for q in range(1, 4):
             nc.sync.dma_start(out=w_planes[q * QUADRANT : q * QUADRANT + 4, :, :], in_=w_planes[4 * q : 4 * q + 4, :, :])
         nc.vector.tensor_copy(v_rows[:], tab_s[:].bitcast(U8).indirect(idx[:]))
@@ -240,8 +240,9 @@ def tile_list_gmu_silu_resL_kernel(
 
         quantise_wt(0)
         av[1] = sb("av1", [P, J], F32, tag="wt_raw_then_av")
-        for t in range(NT - 1):
+        for t in range(2):
             both(product_v, t)
+        product_v(0, 2)
         both(product_t, 0)
         b_turned = bank()
         nc.tensor.transpose(b_turned[:, 0:P], b_rows[:], ident[:])
@@ -249,6 +250,7 @@ def tile_list_gmu_silu_resL_kernel(
         both(product_z, 0)
         mix(0)
         quantise_wt(1)
+        product_v(1, 2)
         both(product_v, 3)
         both(product_t, 1)
         both(product_z, 1)

@@ -24,7 +24,7 @@ BLOCKS = H // P
 QUADRANT = 32
 ROWS = 16
 BANKS = 8
-WT_COLS = N // 2
+WT_PARTS = ((0, 1), (1, 2), (2, 4))
 FP4_TILE = P // 2
 WV_PLANE, ZV_PLANE, ZT_PLANE, PLANES = 0, 2, 4, 5
 
@@ -53,9 +53,10 @@ def tile_list_gmu_silu_resL_kernel(
         wv_w = sb("wv_w", [P, 2, N // 2], I32)
         zv_w = sb("zv_w", [P, 2, N // 2], I32)
         zt_w = sb("zt_w", [P, N // 2], I32)
-        wt_raw = [sb("wt_raw0", [P, 4, WT_COLS], F32, tag="wt_raw_then_av"), sb("wt_raw1", [P, 4, WT_COLS], F32)]
-        wt_bf = [sb(f"wt_bf{c}", [P, WT_COLS, 4], BF16) for c in range(2)]
-        wt_plane = [sb(f"wt_plane{c}", [P, WT_COLS], U8) for c in range(2)]
+        widths = [(end - first) * P for first, end in WT_PARTS]
+        wt_raw = [sb(f"wt_raw{c}", [P, 4, w], F32, tag="wt_raw_then_av" if c == 0 else None) for c, w in enumerate(widths)]
+        wt_bf = [sb(f"wt_bf{c}", [P, w, 4], BF16) for c, w in enumerate(widths)]
+        wt_plane = [sb(f"wt_plane{c}", [P, w], U8) for c, w in enumerate(widths)]
         r_win = [sb(f"r_win{t}", [P, T], F32) for t in range(NT)]
         b_rows = sb("b_rows", [P, P], F32)
         ident = sb("ident", [P, P], F32)
@@ -96,7 +97,7 @@ def tile_list_gmu_silu_resL_kernel(
             nc.sync.dma_start(out=w_planes[0:ROWS, first : first + passes, :], in_=src.rearrange("a g n -> g a n").bitcast(I32))
 
         def load_wt(c):
-            nc.sync.dma_start(out=wt_raw[c][:], in_=wt.rearrange("(p i) n -> p i n", i=4)[:, :, c * WT_COLS : (c + 1) * WT_COLS])
+            nc.sync.dma_start(out=wt_raw[c][:], in_=wt.rearrange("(p i) n -> p i n", i=4)[:, :, WT_PARTS[c][0] * P : WT_PARTS[c][1] * P])
 
         def load_r(t):
             nc.sync.dma_start(out=r_win[t][:], in_=rT[t * P : (t + 1) * P, :])
@@ -126,8 +127,9 @@ def tile_list_gmu_silu_resL_kernel(
         nc.sync.dma_start(out=zv_w[:], in_=zv_words.rearrange("a p n -> p a n").bitcast(I32))
         nc.sync.dma_start(out=zt_w[:], in_=zt_words[0].bitcast(I32))
         nc.sync.dma_start(out=b_rows[0:NT, :], in_=b.rearrange("(t p) -> t p", p=P))
-        load_r(1)
         load_wt(1)
+        load_r(1)
+        load_wt(2)
         load_r(2)
         load_r(3)
 
@@ -164,9 +166,10 @@ def tile_list_gmu_silu_resL_kernel(
 
         def product_t(h, t):
             acc = bank()
-            c = slice((t % 2) * P, (t % 2 + 1) * P)
+            part = min(t, len(WT_PARTS) - 1)
+            c = slice((t - WT_PARTS[part][0]) * P, (t - WT_PARTS[part][0] + 1) * P)
             nc.tensor.matmul_mx(
-                out=acc[:], lhsT=wt_codes[t // 2][:, c].bitcast(FP8X4), lhsT_scale=wt_plane[t // 2][:, c],
+                out=acc[:], lhsT=wt_codes[part][:, c].bitcast(FP8X4), lhsT_scale=wt_plane[part][:, c],
                 rhs=v2_codes[:, half(h)].bitcast(FP8X4), rhs_scale=v2_plane[:, half(h)], start=True, stop=True,
             )
             nc.scalar.activation(at[t][:, half(h)], acc[:], ACT.Silu)
@@ -187,7 +190,7 @@ def tile_list_gmu_silu_resL_kernel(
         nc.vector.tensor_copy(v2_codes[:], tab2_w[:].bitcast(U32).indirect(idx2[:]))
         nc.vector.tensor_copy(v2_plane[:], tab2_s[:].bitcast(U8).indirect(idx2[:]))
 
-        wt_codes = [sb(f"wt_codes{c}", [P, WT_COLS], U32) for c in range(2)]
+        wt_codes = [sb(f"wt_codes{c}", [P, w], U32) for c, w in enumerate(widths)]
 
         def quantise_wt(c):
             nc.scalar.copy(wt_bf[c][:].rearrange("p (m n) i -> p m i n", n=4), wt_raw[c][:].rearrange("p i (m n) -> p m i n", n=4))
@@ -250,6 +253,7 @@ def tile_list_gmu_silu_resL_kernel(
         both(product_z, 0)
         mix(0)
         quantise_wt(1)
+        quantise_wt(2)
         product_v(1, 2)
         both(product_v, 3)
         both(product_t, 1)

@@ -50,7 +50,8 @@ def tile_list_gmu_silu_resL_kernel(
         w_planes = sb("w_planes", [P, PLANES, N // 4], I32)
         tab_w = sb("tab_w", [P, T], I32)
         tab2_w = sb("tab2_w", [P, T], I32)
-        wv_w = sb("wv_w", [P, 2, N // 2], I32)
+        wv_w = sb("wv_w", [P, 2, (NT - 1) * FP4_TILE], I32)
+        wv_last = sb("wv_last", [P, 2, FP4_TILE], I32)
         zv_w = sb("zv_w", [P, 2, N // 2], I32)
         zt_w = sb("zt_w", [P, N // 2], I32)
         widths = [(end - first) * P for first, end in WT_PARTS]
@@ -113,7 +114,8 @@ def tile_list_gmu_silu_resL_kernel(
         load_rows(ZV_PLANE, 2, zv_scales)
         load_rows(ZT_PLANE, 1, zt_scales)
         nc.sync.dma_start(out=tab2_w[:], in_=tab2_words[0].rearrange("p t b -> p (t b)").bitcast(I32))
-        nc.sync.dma_start(out=wv_w[:], in_=wv_words.rearrange("a p n -> p a n").bitcast(I32))
+        wv_view = wv_words.rearrange("a p n -> p a n").bitcast(I32)
+        nc.sync.dma_start(out=wv_w[:], in_=wv_view[:, :, 0 : (NT - 1) * FP4_TILE])
         for q in range(1, 4):
             nc.sync.dma_start(out=w_planes[q * QUADRANT : q * QUADRANT + 4, :, :], in_=w_planes[4 * q : 4 * q + 4, :, :])
         nc.vector.tensor_copy(v_rows[:], tab_s[:].bitcast(U8).indirect(idx[:]))
@@ -128,6 +130,7 @@ def tile_list_gmu_silu_resL_kernel(
         nc.sync.dma_start(out=zt_w[:], in_=zt_words[0].bitcast(I32))
         nc.sync.dma_start(out=b_rows[0:NT, :], in_=b.rearrange("(t p) -> t p", p=P))
         load_wt(1)
+        nc.sync.dma_start(out=wv_last[:], in_=wv_view[:, :, (NT - 1) * FP4_TILE :])
         load_r(1)
         load_wt(2)
         load_r(2)
@@ -153,7 +156,7 @@ def tile_list_gmu_silu_resL_kernel(
         def v_passes(acc, words, first_plane, h, t, stop):
             for a in range(2):
                 nc.tensor.matmul_mx(
-                    out=acc[:], lhsT=words[:, a, t * FP4_TILE : (t + 1) * FP4_TILE].bitcast(FP4X4),
+                    out=acc[:], lhsT=words[:, a, :].bitcast(FP4X4),
                     lhsT_scale=w_plane(first_plane + a, t),
                     rhs=v_codes[h][:, a, :].bitcast(FP4X4), rhs_scale=v_bytes[:, a * J + h * H : a * J + (h + 1) * H],
                     start=(a == 0), stop=(stop and a == 1),
@@ -161,7 +164,7 @@ def tile_list_gmu_silu_resL_kernel(
 
         def product_v(h, t):
             acc = bank()
-            v_passes(acc, wv_w, WV_PLANE, h, t, True)
+            v_passes(acc, wv_last[:] if t == NT - 1 else wv_w[:, :, t * FP4_TILE : (t + 1) * FP4_TILE], WV_PLANE, h, t, True)
             nc.scalar.activation(av[t][:, half(h)], acc[:], ACT.Silu)
 
         def product_t(h, t):
@@ -176,7 +179,7 @@ def tile_list_gmu_silu_resL_kernel(
 
         def product_z(h, t):
             acc = bank()
-            v_passes(acc, zv_w, ZV_PLANE, h, t, False)
+            v_passes(acc, zv_w[:, :, t * FP4_TILE : (t + 1) * FP4_TILE], ZV_PLANE, h, t, False)
             nc.tensor.matmul_mx(
                 out=acc[:], lhsT=zt_w[:, t * FP4_TILE : (t + 1) * FP4_TILE].bitcast(FP4X4), lhsT_scale=w_plane(ZT_PLANE, t),
                 rhs=v2_codes[:, half(h)].bitcast(FP8X4), rhs_scale=v2_plane[:, half(h)], start=False, stop=True,

from contextlib import ExitStack

import concourse.mybir as mybir
from concourse.masks import make_identity

K, L, N, T, J = 1024, 512, 512, 2048, 1024
FLOPS = 2 * N * J * (2 * K + 2 * L)

F32 = mybir.dt.float32
BF16 = mybir.dt.bfloat16
I32 = mybir.dt.int32
U32 = mybir.dt.uint32
U16 = mybir.dt.uint16
U8 = mybir.dt.uint8
FP8X4 = mybir.dt.float8_e4m3fn_x4
FP4X4 = mybir.dt.float4_e2m1fn_x4
ACT = mybir.ActivationFunctionType
ALU = mybir.AluOpType

P = 128
H = 512
NT = N // P
BLOCKS = H // P
QUADRANT = 32
ROWS = 16
BANKS = 8
WT_PARTS = ((0, 1), (1, 2), (2, 4))
FP4_TILE = P // 2
WV_PLANE, ZV_PLANE, ZT_PLANE, PLANES = 0, 2, 4, 5


def tile_list_gmu_silu_resL_kernel(
    tc, tab_words, tab_scales, tab2_words, tab2_scales, zv_words, zv_scales, zt_words, zt_scales,
    b, wv_words, wv_scales, wt, rT, offs, offs2, out,
):
    nc = tc.nc
    with ExitStack() as ctx:
        lists = ctx.enter_context(tc.tile_pool(name="lists", bufs=1))
        keep = ctx.enter_context(tc.tile_pool(name="keep", bufs=1))
        psum = ctx.enter_context(tc.psum_pool(name="psum", bufs=1))

        def sb(name, shape, dtype, tag=None):
            return keep.tile(shape, dtype, name=name, tag=tag or name, align_bytes=64)

        idx = lists.tile([P, J // 16], U16, name="idx")
        idx2 = lists.tile([P, J // 16], U16, name="idx2")

        tab_s = sb("tab_s", [P, T // 4], I32, tag="tab_s_then_planes")
        tab2_s = sb("tab2_s", [P, T // 4], I32)
        w_planes = sb("w_planes", [P, PLANES, N // 4], I32)
        tab_w = sb("tab_w", [P, T], I32)
        tab2_w = sb("tab2_w", [P, T], I32)
        wv_w = sb("wv_w", [P, 2, (NT - 1) * FP4_TILE], I32)
        wv_last = sb("wv_last", [P, 2, FP4_TILE], I32)
        zv_w = sb("zv_w", [P, 2, N // 2], I32)
        zt_w = sb("zt_w", [P, N // 2], I32)
        widths = [(end - first) * P for first, end in WT_PARTS]
        wt_raw = [sb(f"wt_raw{c}", [P, 4, w], F32, tag="wt_raw_then_av" if c == 0 else None) for c, w in enumerate(widths)]
        wt_bf = [sb(f"wt_bf{c}", [P, w, 4], BF16) for c, w in enumerate(widths)]
        wt_plane = [sb(f"wt_plane{c}", [P, w], U8) for c, w in enumerate(widths)]
        r_win = [sb(f"r_win{t}", [P, T], F32) for t in range(NT)]
        b_rows = sb("b_rows", [P, P], F32)
        ident = sb("ident", [P, P], F32)
        b_half = sb("b_half", [P, NT], F32)

        warm_in = sb("warm_in", [P, 8], F32)
        warm_out = sb("warm_out", [P, 8], F32)

        v_rows = sb("v_rows", [P, J], U8)
        v_pairs = sb("v_pairs", [P, J], U32)
        v_codes = [sb(f"v_codes{h}", [P, 2, H], U16) for h in range(2)]
        v2_codes = sb("v2_codes", [P, J], U32)
        v2_plane = sb("v2_plane", [P, J], U8)

        def row_tiles(name):
            return [sb(f"{name}{t}", [P, J], F32) for t in range(NT)]

        at, th, base, res = [row_tiles(x) for x in ("at", "th", "base", "res")]
        av = {t: sb(f"av{t}", [P, J], F32) for t in (0, 2, 3)}
        turned = [sb(f"turned{t}", [P, J], F32) for t in range(2)]
        diff = at
        prod = th

        def zero_on_vector(rows):
            cut = rows.shape[1] // 2 + 1
            nc.vector.memset(rows[:, 0:cut], 0)
            nc.vector.memset(rows[:, cut:], 0)

        nc.gpsimd.memset(tab2_s[:], 0)
        zero_on_vector(w_planes[:].rearrange("p a n -> p (a n)"))
        zero_on_vector(tab_s[QUADRANT : 2 * QUADRANT, :])
        zero_on_vector(tab_s[2 * QUADRANT : P, :])
        nc.vector.memset(warm_in[:], 0.0)
        nc.scalar.activation(warm_out[:], warm_in[:], ACT.Silu)
        nc.vector.memset(b_rows[:], 0.0)

        def load_rows(first, passes, src):
            nc.sync.dma_start(out=w_planes[0:ROWS, first : first + passes, :], in_=src.rearrange("a g n -> g a n").bitcast(I32))

        def load_wt(c):
            nc.sync.dma_start(out=wt_raw[c][:], in_=wt.rearrange("(p i) n -> p i n", i=4)[:, :, WT_PARTS[c][0] * P : WT_PARTS[c][1] * P])

        def load_r(t):
            nc.sync.dma_start(out=r_win[t][:], in_=rT[t * P : (t + 1) * P, :])

        nc.sync.dma_start(idx[:], offs)
        nc.sync.dma_start(out=tab_s[0 : 2 * ROWS, :], in_=tab_scales.rearrange("a g t -> g a t").bitcast(I32))
        nc.sync.dma_start(out=tab_w[:], in_=tab_words[0].rearrange("p t b -> p (t b)").bitcast(I32))
        nc.sync.dma_start(idx2[:], offs2)
        tab2_rows = tab2_scales[0].rearrange("(q r) t -> r q t", r=4)
        for r in range(2):
            nc.gpsimd.dma_start(out=tab2_s[r:P:QUADRANT, :], in_=tab2_rows[r].bitcast(I32))
        load_rows(WV_PLANE, 2, wv_scales)
        load_rows(ZV_PLANE, 2, zv_scales)
        load_rows(ZT_PLANE, 1, zt_scales)
        nc.sync.dma_start(out=tab2_w[:], in_=tab2_words[0].rearrange("p t b -> p (t b)").bitcast(I32))
        wv_view = wv_words.rearrange("a p n -> p a n").bitcast(I32)
        nc.sync.dma_start(out=wv_w[:], in_=wv_view[:, :, 0 : (NT - 1) * FP4_TILE])
        for q in range(1, 4):
            nc.sync.dma_start(out=w_planes[q * QUADRANT : q * QUADRANT + 4, :, :], in_=w_planes[4 * q : 4 * q + 4, :, :])
        nc.vector.tensor_copy(v_rows[:], tab_s[:].bitcast(U8).indirect(idx[:]))
        v_planes = sb("v_planes", [P, 2, J // 4], I32, tag="tab_s_then_planes")
        for q in range(4):
            nc.sync.dma_start(out=v_planes[q * QUADRANT : q * QUADRANT + 4, :, :], in_=v_rows[8 * q : 8 * q + 8, :].bitcast(I32))
        for r in range(2, 4):
            nc.sync.dma_start(out=tab2_s[r:P:QUADRANT, :], in_=tab2_rows[r].bitcast(I32))
        load_wt(0)
        load_r(0)
        nc.sync.dma_start(out=zv_w[:], in_=zv_words.rearrange("a p n -> p a n").bitcast(I32))
        nc.sync.dma_start(out=zt_w[:], in_=zt_words[0].bitcast(I32))
        nc.sync.dma_start(out=b_rows[0:NT, :], in_=b.rearrange("(t p) -> t p", p=P))
        load_wt(1)
        nc.sync.dma_start(out=wv_last[:], in_=wv_view[:, :, (NT - 1) * FP4_TILE :])
        load_r(1)
        load_wt(2)
        load_r(2)
        load_r(3)

        make_identity(nc, ident[:])

        w_bytes = w_planes[:].rearrange("p a n -> p (a n)").bitcast(U8)
        v_bytes = v_planes[:].rearrange("p a n -> p (a n)").bitcast(U8)

        def w_plane(place, t):
            return w_bytes[:, place * N + t * P : place * N + (t + 1) * P]

        def half(h):
            return slice(h * H, (h + 1) * H)

        def list_half(h):
            return slice(h * (H // 16), (h + 1) * (H // 16))

        def bank():
            return psum.tile([P, H], F32, name="acc", tag="acc", bufs=BANKS)

        def v_passes(acc, words, first_plane, h, t, stop):
            for a in range(2):
                nc.tensor.matmul_mx(
                    out=acc[:], lhsT=words[:, a, :].bitcast(FP4X4),
                    lhsT_scale=w_plane(first_plane + a, t),
                    rhs=v_codes[h][:, a, :].bitcast(FP4X4), rhs_scale=v_bytes[:, a * J + h * H : a * J + (h + 1) * H],
                    start=(a == 0), stop=(stop and a == 1),
                )

        def product_v(h, t):
            acc = bank()
            v_passes(acc, wv_last[:] if t == NT - 1 else wv_w[:, :, t * FP4_TILE : (t + 1) * FP4_TILE], WV_PLANE, h, t, True)
            nc.scalar.activation(av[t][:, half(h)], acc[:], ACT.Silu)

        def product_t(h, t):
            acc = bank()
            part = min(t, len(WT_PARTS) - 1)
            c = slice((t - WT_PARTS[part][0]) * P, (t - WT_PARTS[part][0] + 1) * P)
            nc.tensor.matmul_mx(
                out=acc[:], lhsT=wt_codes[part][:, c].bitcast(FP8X4), lhsT_scale=wt_plane[part][:, c],
                rhs=v2_codes[:, half(h)].bitcast(FP8X4), rhs_scale=v2_plane[:, half(h)], start=True, stop=True,
            )
            nc.scalar.activation(at[t][:, half(h)], acc[:], ACT.Silu)

        def product_z(h, t):
            acc = bank()
            v_passes(acc, zv_w[:, :, t * FP4_TILE : (t + 1) * FP4_TILE], ZV_PLANE, h, t, False)
            nc.tensor.matmul_mx(
                out=acc[:], lhsT=zt_w[:, t * FP4_TILE : (t + 1) * FP4_TILE].bitcast(FP4X4), lhsT_scale=w_plane(ZT_PLANE, t),
                rhs=v2_codes[:, half(h)].bitcast(FP8X4), rhs_scale=v2_plane[:, half(h)], start=False, stop=True,
            )
            nc.scalar.activation(th[t][:, half(h)], acc[:], ACT.Tanh, bias=b_half[:, t : t + 1], scale=0.5)

        for h in range(2):
            nc.vector.tensor_copy(v_pairs[:, half(h)], tab_w[:].bitcast(U32).indirect(idx[:, list_half(h)]))
        for h in range(2):
            nc.vector.tensor_copy(v_codes[h][:], v_pairs[:, half(h)].bitcast(U16).rearrange("p (t a) -> p a t", a=2))
        nc.vector.tensor_copy(v2_codes[:], tab2_w[:].bitcast(U32).indirect(idx2[:]))
        nc.vector.tensor_copy(v2_plane[:], tab2_s[:].bitcast(U8).indirect(idx2[:]))

        wt_codes = [sb(f"wt_codes{c}", [P, w], U32) for c, w in enumerate(widths)]

        def quantise_wt(c):
            nc.scalar.copy(wt_bf[c][:].rearrange("p (m n) i -> p m i n", n=4), wt_raw[c][:].rearrange("p i (m n) -> p m i n", n=4))
            nc.vector.quantize_mx(out=wt_codes[c][:].bitcast(FP8X4), scales=wt_plane[c][:], in_=wt_bf[c][:].rearrange("p n i -> p (n i)"))

        def both(step, t):
            for h in range(2):
                step(h, t)

        def product(t, c):
            nc.vector.scalar_tensor_tensor(prod[t][:, c], th[t][:, c], -1.0, diff[t][:, c], ALU.add, ALU.mult)

        def mix(t):
            nc.vector.tensor_tensor(base[t][:], r_win[t][:].indirect(idx[:]), av[t][:], ALU.add)
            for h in range(2):
                nc.vector.tensor_tensor(diff[t][:, half(h)], av[t][:, half(h)], at[t][:, half(h)], ALU.subtract)
            if t < NT - 1:
                for h in range(2):
                    product(t, half(h))

        def finish_on_vector(t, c):
            nc.vector.scalar_tensor_tensor(res[t][:, c], prod[t][:, c], 0.5, base[t][:, c], ALU.mult, ALU.add)
            nc.sync.dma_start(out=out[t * P : (t + 1) * P, c], in_=res[t][:, c])

        def sum_turned(h, t):
            acc = bank()
            for s in range(BLOCKS):
                c = slice(s * P, (s + 1) * P)
                j = slice(h * H + s * P, h * H + (s + 1) * P)
                nc.tensor.matmul(acc[:, c], base[t][:, j], ident[:], start=True, stop=False, is_transpose=True)
                nc.tensor.matmul(acc[:, c], base[t][:, j], ident[:], start=False, stop=False, is_transpose=True)
                nc.tensor.matmul(acc[:, c], prod[t][:, j], ident[:], start=False, stop=True, is_transpose=True)
            nc.scalar.activation(turned[t][:, half(h)], acc[:], ACT.Copy, scale=0.5)

        def turn_back(h, t):
            acc = bank()
            for s in range(BLOCKS):
                j = slice(h * H + s * P, h * H + (s + 1) * P)
                nc.tensor.transpose(acc[:, s * P : (s + 1) * P], turned[t][:, j], ident[:])
            nc.scalar.copy(res[t][:, half(h)], acc[:])
            nc.sync.dma_start(out=out[t * P : (t + 1) * P, half(h)], in_=res[t][:, half(h)])

        def last_tile():
            pieces = (half(0), slice(H, H + H // 2), slice(H + H // 2, J))
            product(NT - 1, pieces[0])
            for n, c in enumerate(pieces):
                if n + 1 < len(pieces):
                    product(NT - 1, pieces[n + 1])
                finish_on_vector(NT - 1, c)

        quantise_wt(0)
        av[1] = sb("av1", [P, J], F32, tag="wt_raw_then_av")
        for t in range(2):
            both(product_v, t)
        product_v(0, 2)
        both(product_t, 0)
        b_turned = bank()
        nc.tensor.transpose(b_turned[:, 0:P], b_rows[:], ident[:])
        nc.scalar.activation(b_half[:], b_turned[:, 0:NT], ACT.Copy, scale=0.5)
        both(product_z, 0)
        mix(0)
        quantise_wt(1)
        quantise_wt(2)
        product_v(1, 2)
        both(product_v, 3)
        both(product_t, 1)
        both(product_z, 1)
        mix(1)
        both(sum_turned, 0)
        product_z(0, 2)
        both(turn_back, 0)
        product_z(1, 2)
        both(product_t, 2)
        mix(2)
        for h in range(2):
            finish_on_vector(2, half(h))
        both(sum_turned, 1)
        both(product_t, 3)
        both(turn_back, 1)
        product_z(0, 3)
        product_z(1, 3)
        mix(3)
        last_tile()
